import numpy as np
import ml_dtypes


def mxq(x, axis, fmt="e4m3"):
    dtype, down = {"e4m3": (ml_dtypes.float8_e4m3fn, 7), "e5m2": (ml_dtypes.float8_e5m2, 14)}[fmt]
    v = np.moveaxis(np.asarray(x, np.float32).astype(ml_dtypes.bfloat16).astype(np.float64), axis, -1)
    blocks = v.reshape(v.shape[:-1] + (-1, 32))
    amax = np.abs(blocks).max(-1, keepdims=True)
    byte = np.maximum(np.where(amax > 0, np.frexp(amax)[1] - 1 + 127, 0) - down, 1)
    scale = np.exp2(byte - 127.0)
    codes = (blocks / scale).astype(np.float32).astype(dtype).astype(np.float64)
    return np.moveaxis((codes * scale).reshape(v.shape), -1, axis)


WIDE = False


def mx_kscale(k):
    if not WIDE:
        return np.ones(k)
    levels = np.array([10, -10, 5, -5, 0])
    if k % 512:
        return np.exp2(np.random.permutation(np.resize(levels, k // 32))).repeat(32)
    a = np.empty((k // 512, 16))
    for p in range(k // 512):
        a[p, :8] = np.random.permutation(np.resize(levels, 8))
        for g in range(8):
            far = levels[np.abs(levels - a[p, g]) >= 10]
            a[p, g + 8] = far[np.random.randint(len(far))]
    return np.exp2(a.ravel()).repeat(32)


def f64(x):
    return np.asarray(x).astype(np.float64)


def striped(idx):
    return np.tile(idx.reshape(-1, 16).T, (8, 1)).astype(np.uint16)


def unstriped(offs):
    return offs[:16].T.reshape(-1).astype(np.int64)


E2M1 = np.array([0.0, 0.5, 1.0, 1.5, 2.0, 3.0, 4.0, 6.0, -0.0, -0.5, -1.0, -1.5, -2.0, -3.0, -4.0, -6.0])


def pack_weight(w, fmt):
    k, n = w.shape
    w = f64(np.asarray(w, np.float32).astype(ml_dtypes.bfloat16)).reshape(k // 32, 32, n)
    amax = np.abs(w).max(1)
    if fmt == "e4m3":
        byte = np.frexp(amax)[1] - 1 + 127 - 7
    else:
        mant, ex = np.frexp(amax / 6.0)
        byte = np.where(mant > 0.5, ex, ex - 1) + 127
    byte = np.clip(np.where(amax > 0, byte, 1), 1, 254)
    scaled = (w * np.exp2(127.0 - byte)[:, None, :]).reshape(k, n).astype(np.float32)
    by_word = np.ascontiguousarray(scaled.reshape(k // 512, 128, 4, n).transpose(0, 1, 3, 2))
    if fmt == "e4m3":
        words = by_word.astype(ml_dtypes.float8_e4m3fn).view(np.uint8)
    else:
        c = by_word.astype(ml_dtypes.float4_e2m1fn).view(np.uint8) & 0xF
        words = (c[..., 0::2] | (c[..., 1::2] << 4)).reshape(k // 512, 128, 2 * n)
    return np.ascontiguousarray(words), np.ascontiguousarray(byte.astype(np.uint8).reshape(k // 512, 16, n))


def unpack_weight(words, scales, fmt):
    g, _, n = scales.shape
    words = np.ascontiguousarray(words).reshape(g, 128, n, -1)
    if fmt == "e4m3":
        vals = words.view(ml_dtypes.float8_e4m3fn).astype(np.float64)
    else:
        nib = np.empty((g, 128, n, 4), np.uint8)
        nib[..., 0::2] = words & 0xF
        nib[..., 1::2] = words >> 4
        vals = E2M1[nib]
    vals = vals * np.repeat(np.exp2(scales.astype(np.float64) - 127.0), 8, axis=1)[..., None]
    return vals.transpose(0, 1, 3, 2).reshape(g * 512, n)


K, T, E, C, N = 256, 1024, 2, 256, 512


def by_expert(wq, xq):
    return np.concatenate([wq[e].T @ xq[:, e * C:(e + 1) * C] for e in range(E)], axis=1)


def setup_inputs():
    n = np.random.standard_normal
    v = mx_kscale(N)
    slot_token = np.random.permutation(T)[:E * C]
    w_slot = np.random.uniform(0.2, 1.0, E * C)
    dq = pack_weight(n((N, T)) * v[:, None], "e4m3")
    dk = pack_weight(n((N, T)) * v[:, None], "e4m3")
    dv = pack_weight(n((N, T)) * v[:, None], "e4m3")
    wq = [pack_weight(m, "e4m3") for m in n((E, N, K)) / np.sqrt(N) / v[None, :, None]]
    wv = [pack_weight(m, "e2m1") for m in n((E, N, K)) / np.sqrt(N) / v[None, :, None]]
    return {
        "dq_words": dq[0],
        "dq_scales": dq[1],
        "dk_words": dk[0],
        "dk_scales": dk[1],
        "dv_words": dv[0],
        "dv_scales": dv[1],
        "wq_words": np.stack([m[0] for m in wq]),
        "wq_scales": np.stack([m[1] for m in wq]),
        "wk": (n((E, N, K)) / np.sqrt(N) / v[None, :, None]).astype(np.float32),
        "wv_words": np.stack([m[0] for m in wv]),
        "wv_scales": np.stack([m[1] for m in wv]),
        "gate": (np.tile(w_slot, (128, 1))).astype(np.float32),
        "offs": striped(slot_token),
    }


def reference(dq_words, dq_scales, dk_words, dk_scales, dv_words, dv_scales, wq_words, wq_scales, wk, wv_words, wv_scales, gate, offs):
    wq = np.stack([unpack_weight(wq_words[e], wq_scales[e], "e4m3") for e in range(E)])
    wkq = mxq(f64(wk), 1, "e4m3")
    wv = np.stack([unpack_weight(wv_words[e], wv_scales[e], "e2m1") for e in range(E)])
    idx = unstriped(offs)
    gq, gk, gv = [unpack_weight(w, s, "e4m3")[:, idx] for w, s in ((dq_words, dq_scales), (dk_words, dk_scales), (dv_words, dv_scales))]
    dx = f64(gate[:1]) * (by_expert(wq, gq) + by_expert(wkq, gk) + by_expert(wv, gv))
    out = np.zeros((K, T))
    out[:, idx] = dx
    return out

@@ -1,0 +1,131 @@
+from contextlib import ExitStack
+
+import concourse.mybir as mybir
+
+K, T, E, C, N = 256, 1024, 2, 256, 512
+FLOPS = 3 * 2 * N * K * E * C
+
+F32 = mybir.dt.float32
+BF16 = mybir.dt.bfloat16
+I32 = mybir.dt.int32
+U32 = mybir.dt.uint32
+U16 = mybir.dt.uint16
+U8 = mybir.dt.uint8
+FP8X4 = mybir.dt.float8_e4m3fn_x4
+FP4X4 = mybir.dt.float4_e2m1fn_x4
+MULT = mybir.AluOpType.mult
+
+P = 128
+PACK = 4
+QUAD = 32
+BLOCKS = K // P
+LIST_COLS = C // 16
+
+
+def tile_moe_qkb_kernel(tc, dq_words, dq_scales, dk_words, dk_scales, dv_words, dv_scales, wq_words, wq_scales, wk, wv_words, wv_scales, gate, offs, out):
+    nc = tc.nc
+    with ExitStack() as ctx:
+        keep = ctx.enter_context(tc.tile_pool(name="keep", bufs=1))
+        psum = ctx.enter_context(tc.psum_pool(name="psum", bufs=1))
+
+        def tile(shape, dtype, name):
+            return keep.tile(shape, dtype, name=name, align_bytes=64)
+
+        offsets = keep.tile([P, E * LIST_COLS], U16, name="offsets")
+        table_w = {g: tile([P, T], U32, "table_w_" + g) for g in "qkv"}
+        table_s = {g: tile([P, T], U8, "table_s_" + g) for g in "qkv"}
+        wq_w = tile([P, E, K], U32, "wq_w")
+        wq_s = tile([P, E, K], U8, "wq_s")
+        wv_w = tile([P, E, 2 * K], U8, "wv_w")
+        wv_s = tile([P, E, K], U8, "wv_s")
+        wk_raw = [tile([P, PACK, K], F32, "wk_raw%d" % e) for e in range(E)]
+        wk_bf = [tile([P, K, PACK], BF16, "wk_bf%d" % e) for e in range(E)]
+        wk_w = [tile([P, K], U32, "wk_w%d" % e) for e in range(E)]
+        wk_s = [tile([P, K], U8, "wk_s%d" % e) for e in range(E)]
+        gates = tile([P, E * C], F32, "gates")
+        result = [tile([P, T], F32, "result%d" % b) for b in range(BLOCKS)]
+
+        for g in "qvk":
+            nc.vector.memset(table_s[g][:].bitcast(I32), 0)
+        zero = tile([P, 8], F32, "zero")
+        nc.vector.memset(zero[:], 0.0)
+        for b in range(BLOCKS):
+            nc.scalar.copy(out=result[b][:], in_=zero[:, 0:1].to_broadcast([P, T]))
+
+        def load_table_words(queue, g, words):
+            queue.dma_start(out=table_w[g][:].bitcast(I32), in_=words[0].rearrange("p t d -> p (t d)").bitcast(I32))
+
+        def load_table_scales(queue, g, scales):
+            rows = scales[0].rearrange("(q r) t -> r q t", r=4)
+            for r in range(4):
+                queue.dma_start(out=table_s[g][r:P:QUAD, :].bitcast(I32), in_=rows[r].bitcast(I32))
+
+        def load_weight_scales(queue, plane, scales):
+            rows = scales.rearrange("e s (q r) c -> r q (e s) c", r=4)
+            for r in range(4):
+                queue.dma_start(out=plane[r:P:QUAD, :, :].bitcast(I32), in_=rows[r].bitcast(I32))
+
+        def load_wk(queue, e):
+            queue.dma_start(out=wk_raw[e][:], in_=wk[e].rearrange("(p j) c -> p j c", j=PACK))
+
+        nc.sync.dma_start(offsets[:], offs)
+        load_table_words(nc.sync, "q", dq_words)
+        load_table_words(nc.sync, "v", dv_words)
+        load_table_scales(nc.sync, "q", dq_scales)
+        load_wk(nc.sync, 0)
+        load_table_scales(nc.sync, "v", dv_scales)
+        load_table_words(nc.sync, "k", dk_words)
+        load_table_scales(nc.sync, "k", dk_scales)
+        load_weight_scales(nc.gpsimd, wq_s, wq_scales)
+        nc.sync.dma_start(out=wq_w[:].bitcast(I32), in_=wq_words.rearrange("e s p c d -> p (e s) (c d)").bitcast(I32))
+        nc.sync.dma_start(out=wv_w[:].bitcast(I32), in_=wv_words.rearrange("e s p b -> p (e s) b").bitcast(I32))
+        load_wk(nc.sync, 1)
+        load_weight_scales(nc.sync, wv_s, wv_scales)
+        nc.sync.dma_start(out=gates[:], in_=gate)
+
+        def gather(table, dtype, name, lo, hi):
+            slots = tile([P, (hi - lo) * C], dtype, name)
+            nc.vector.tensor_copy(slots[:], table[:].indirect(offsets[:, lo * LIST_COLS : hi * LIST_COLS]))
+            return slots
+
+        def quantize_wk(e):
+            nc.scalar.copy(
+                out=wk_bf[e][:].rearrange("p (c i) j -> p c j i", i=4),
+                in_=wk_raw[e][:].rearrange("p j (c i) -> p c j i", i=4),
+            )
+            nc.vector.quantize_mx(out=wk_w[e][:].bitcast(FP8X4), scales=wk_s[e][:], in_=wk_bf[e][:].rearrange("p c j -> p (c j)"))
+
+        q_w = gather(table_w["q"], U32, "q_w", 0, E)
+        v_w = gather(table_w["v"], U32, "v_w", 0, E)
+        q_s = gather(table_s["q"], U8, "q_s", 0, E)
+        v_s = gather(table_s["v"], U8, "v_s", 0, E)
+        quantize_wk(0)
+        k_w, k_s = [], []
+        for e in range(E):
+            k_w.append(gather(table_w["k"], U32, "k_w%d" % e, e, e + 1))
+            k_s.append(gather(table_s["k"], U8, "k_s%d" % e, e, e + 1))
+        quantize_wk(1)
+
+        for e in range(E):
+            slots = slice(e * C, (e + 1) * C)
+            sums = [psum.tile([P, C], F32, name="sums%d_%d" % (e, b)) for b in range(BLOCKS)]
+            for b in range(BLOCKS):
+                cols = slice(b * P, (b + 1) * P)
+                nc.tensor.matmul_mx(out=sums[b][:], lhsT=wq_w[:, e, cols].bitcast(FP8X4), lhsT_scale=wq_s[:, e, cols],
+                                    rhs=q_w[:, slots].bitcast(FP8X4), rhs_scale=q_s[:, slots], start=True, stop=False)
+                for h in range(C // P):
+                    half = slice(e * C + h * P, e * C + (h + 1) * P)
+                    nc.tensor.matmul_mx(out=sums[b][:, h * P : (h + 1) * P], lhsT=wv_w[:, e, 2 * b * P : 2 * (b + 1) * P].bitcast(FP4X4),
+                                        lhsT_scale=wv_s[:, e, cols], rhs=v_w[:, half].bitcast(FP8X4), rhs_scale=v_s[:, half],
+                                        start=False, stop=False)
+            for b in range(BLOCKS):
+                cols = slice(b * P, (b + 1) * P)
+                nc.tensor.matmul_mx(out=sums[b][:], lhsT=wk_w[e][:, cols].bitcast(FP8X4), lhsT_scale=wk_s[e][:, cols],
+                                    rhs=k_w[e][:].bitcast(FP8X4), rhs_scale=k_s[e][:], start=False, stop=True)
+            for b in range(BLOCKS):
+                dx = tile([P, C], F32, "dx%d_%d" % (e, b))
+                nc.scalar.copy(out=dx[:], in_=sums[b][:])
+                nc.vector.tensor_tensor(result[b][:].indirect(offsets[:, e * LIST_COLS : (e + 1) * LIST_COLS]), dx[:], gates[:, slots], MULT)
+
+        for b in range(BLOCKS):
+            nc.sync.dma_start(out=out[b * P : (b + 1) * P, :], in_=result[b][:])

@@ -20,6 +20,7 @@ PACK = 4
 QUAD = 32
 BLOCKS = K // P
 LIST_COLS = C // 16
+FIRST_ROW = {"q": 4, "k": 12, "v": 0, "wq": 8, "wv": 0}
 
 
 def tile_moe_qkb_kernel(tc, dq_words, dq_scales, dk_words, dk_scales, dv_words, dv_scales, wq_words, wq_scales, wk, wv_words, wv_scales, gate, offs, out):
@@ -58,12 +59,12 @@ def tile_moe_qkb_kernel(tc, dq_words, dq_scales, dk_words, dk_scales, dv_words, 
         def load_table_scales(queue, g, scales):
             rows = scales[0].rearrange("(q r) t -> r q t", r=4)
             for r in range(4):
-                queue.dma_start(out=table_s[g][r:P:QUAD, :].bitcast(I32), in_=rows[r].bitcast(I32))
+                queue.dma_start(out=table_s[g][FIRST_ROW[g] + r : P : QUAD, :].bitcast(I32), in_=rows[r].bitcast(I32))
 
-        def load_weight_scales(queue, plane, scales):
+        def load_weight_scales(queue, plane, scales, first):
             rows = scales.rearrange("e s (q r) c -> r q (e s) c", r=4)
             for r in range(4):
-                queue.dma_start(out=plane[r:P:QUAD, :, :].bitcast(I32), in_=rows[r].bitcast(I32))
+                queue.dma_start(out=plane[first + r : P : QUAD, :, :].bitcast(I32), in_=rows[r].bitcast(I32))
 
         def load_wk(queue, e):
             queue.dma_start(out=wk_raw[e][:], in_=wk[e].rearrange("(p j) c -> p j c", j=PACK))
@@ -76,11 +77,11 @@ def tile_moe_qkb_kernel(tc, dq_words, dq_scales, dk_words, dk_scales, dv_words, 
         load_table_scales(nc.sync, "v", dv_scales)
         load_table_words(nc.sync, "k", dk_words)
         load_table_scales(nc.sync, "k", dk_scales)
-        load_weight_scales(nc.gpsimd, wq_s, wq_scales)
+        load_weight_scales(nc.gpsimd, wq_s, wq_scales, FIRST_ROW["wq"])
         nc.sync.dma_start(out=wq_w[:].bitcast(I32), in_=wq_words.rearrange("e s p c d -> p (e s) (c d)").bitcast(I32))
         nc.sync.dma_start(out=wv_w[:].bitcast(I32), in_=wv_words.rearrange("e s p b -> p (e s) b").bitcast(I32))
         load_wk(nc.sync, 1)
-        load_weight_scales(nc.sync, wv_s, wv_scales)
+        load_weight_scales(nc.sync, wv_s, wv_scales, FIRST_ROW["wv"])
         nc.sync.dma_start(out=gates[:], in_=gate)
 
         def gather(table, dtype, name, lo, hi):
@@ -111,17 +112,15 @@ def tile_moe_qkb_kernel(tc, dq_words, dq_scales, dk_words, dk_scales, dv_words, 
             sums = [psum.tile([P, C], F32, name="sums%d_%d" % (e, b)) for b in range(BLOCKS)]
             for b in range(BLOCKS):
                 cols = slice(b * P, (b + 1) * P)
-                nc.tensor.matmul_mx(out=sums[b][:], lhsT=wq_w[:, e, cols].bitcast(FP8X4), lhsT_scale=wq_s[:, e, cols],
-                                    rhs=q_w[:, slots].bitcast(FP8X4), rhs_scale=q_s[:, slots], start=True, stop=False)
+                nc.tensor.matmul_mx(out=sums[b][:], lhsT=wq_w[:, e, cols].bitcast(FP8X4), lhsT_scale=wq_s[FIRST_ROW["wq"] :, e, cols],
+                                    rhs=q_w[:, slots].bitcast(FP8X4), rhs_scale=q_s[FIRST_ROW["q"] :, slots], start=True, stop=False)
                 for h in range(C // P):
                     half = slice(e * C + h * P, e * C + (h + 1) * P)
                     nc.tensor.matmul_mx(out=sums[b][:, h * P : (h + 1) * P], lhsT=wv_w[:, e, 2 * b * P : 2 * (b + 1) * P].bitcast(FP4X4),
                                         lhsT_scale=wv_s[:, e, cols], rhs=v_w[:, half].bitcast(FP8X4), rhs_scale=v_s[:, half],
                                         start=False, stop=False)
-            for b in range(BLOCKS):
-                cols = slice(b * P, (b + 1) * P)
                 nc.tensor.matmul_mx(out=sums[b][:], lhsT=wk_w[e][:, cols].bitcast(FP8X4), lhsT_scale=wk_s[e][:, cols],
-                                    rhs=k_w[e][:].bitcast(FP8X4), rhs_scale=k_s[e][:], start=False, stop=True)
+                                    rhs=k_w[e][:].bitcast(FP8X4), rhs_scale=k_s[e][FIRST_ROW["k"] :, :], start=False, stop=True)
             for b in range(BLOCKS):
                 dx = tile([P, C], F32, "dx%d_%d" % (e, b))
                 nc.scalar.copy(out=dx[:], in_=sums[b][:])

@@ -40,18 +40,18 @@ def tile_moe_qkb_kernel(tc, dq_words, dq_scales, dk_words, dk_scales, dv_words, 
         wv_w = tile([P, E, 2 * K], U8, "wv_w")
         wv_s = tile([P, E, K], U8, "wv_s")
         wk_raw = [tile([P, PACK, K], F32, "wk_raw%d" % e) for e in range(E)]
-        wk_bf = [tile([P, K, PACK], BF16, "wk_bf%d" % e) for e in range(E)]
         wk_w = [tile([P, K], U32, "wk_w%d" % e) for e in range(E)]
         wk_s = [tile([P, K], U8, "wk_s%d" % e) for e in range(E)]
-        gates = tile([P, E * C], F32, "gates")
-        result = [tile([P, T], F32, "result%d" % b) for b in range(BLOCKS)]
+        gates = [tile([P, C], F32, "gates%d" % e) for e in range(E)]
+        result = [tile([P, T], F32, "result0"), tile([P, T + K * PACK // 2], F32, "result1")]
+        wk_bf = [tile([P, K * PACK], BF16, "wk_bf0")[:], result[1][:, T:].bitcast(BF16)]
 
         for g in "qvk":
             nc.vector.memset(table_s[g][:].bitcast(I32), 0)
         zero = tile([P, 8], F32, "zero")
         nc.vector.memset(zero[:], 0.0)
         for b in range(BLOCKS):
-            nc.scalar.copy(out=result[b][:], in_=zero[:, 0:1].to_broadcast([P, T]))
+            nc.scalar.copy(out=result[b][:, 0:T], in_=zero[:, 0:1].to_broadcast([P, T]))
 
         def load_table_words(queue, g, words):
             queue.dma_start(out=table_w[g][:].bitcast(I32), in_=words[0].rearrange("p t d -> p (t d)").bitcast(I32))
@@ -71,8 +71,8 @@ def tile_moe_qkb_kernel(tc, dq_words, dq_scales, dk_words, dk_scales, dv_words, 
 
         nc.sync.dma_start(offsets[:], offs)
         load_table_words(nc.sync, "q", dq_words)
-        load_table_words(nc.sync, "v", dv_words)
         load_table_scales(nc.sync, "q", dq_scales)
+        load_table_words(nc.sync, "v", dv_words)
         load_wk(nc.sync, 0)
         load_table_scales(nc.sync, "v", dv_scales)
         load_table_words(nc.sync, "k", dk_words)
@@ -80,9 +80,10 @@ def tile_moe_qkb_kernel(tc, dq_words, dq_scales, dk_words, dk_scales, dv_words, 
         load_weight_scales(nc.gpsimd, wq_s, wq_scales, FIRST_ROW["wq"])
         nc.sync.dma_start(out=wq_w[:].bitcast(I32), in_=wq_words.rearrange("e s p c d -> p (e s) (c d)").bitcast(I32))
         nc.sync.dma_start(out=wv_w[:].bitcast(I32), in_=wv_words.rearrange("e s p b -> p (e s) b").bitcast(I32))
-        load_wk(nc.sync, 1)
         load_weight_scales(nc.sync, wv_s, wv_scales, FIRST_ROW["wv"])
-        nc.sync.dma_start(out=gates[:], in_=gate)
+        nc.sync.dma_start(out=gates[0][:], in_=gate[:, 0:C])
+        load_wk(nc.sync, 1)
+        nc.sync.dma_start(out=gates[1][:], in_=gate[:, C : 2 * C])
 
         def gather(table, dtype, name, lo, hi):
             slots = tile([P, (hi - lo) * C], dtype, name)
@@ -91,40 +92,41 @@ def tile_moe_qkb_kernel(tc, dq_words, dq_scales, dk_words, dk_scales, dv_words, 
 
         def quantize_wk(e):
             nc.scalar.copy(
-                out=wk_bf[e][:].rearrange("p (c i) j -> p c j i", i=4),
+                out=wk_bf[e].rearrange("p (c i j) -> p c j i", i=4, j=PACK),
                 in_=wk_raw[e][:].rearrange("p j (c i) -> p c j i", i=4),
             )
-            nc.vector.quantize_mx(out=wk_w[e][:].bitcast(FP8X4), scales=wk_s[e][:], in_=wk_bf[e][:].rearrange("p c j -> p (c j)"))
+            nc.vector.quantize_mx(out=wk_w[e][:].bitcast(FP8X4), scales=wk_s[e][:], in_=wk_bf[e])
 
         q_w = gather(table_w["q"], U32, "q_w", 0, E)
-        v_w = gather(table_w["v"], U32, "v_w", 0, E)
         q_s = gather(table_s["q"], U8, "q_s", 0, E)
+        v_w = gather(table_w["v"], U32, "v_w", 0, E)
         v_s = gather(table_s["v"], U8, "v_s", 0, E)
         quantize_wk(0)
         k_w, k_s = [], []
-        for e in range(E):
-            k_w.append(gather(table_w["k"], U32, "k_w%d" % e, e, e + 1))
-            k_s.append(gather(table_s["k"], U8, "k_s%d" % e, e, e + 1))
-        quantize_wk(1)
+        k_w.append(gather(table_w["k"], U32, "k_w0", 0, 1))
+        k_s.append(gather(table_s["k"], U8, "k_s0", 0, 1))
+        k_s.append(gather(table_s["k"], U8, "k_s1", 1, 2))
+        k_w.append(gather(table_w["k"], U32, "table_s_k", 1, 2))
 
         for e in range(E):
             slots = slice(e * C, (e + 1) * C)
-            sums = [psum.tile([P, C], F32, name="sums%d_%d" % (e, b)) for b in range(BLOCKS)]
             for b in range(BLOCKS):
                 cols = slice(b * P, (b + 1) * P)
-                nc.tensor.matmul_mx(out=sums[b][:], lhsT=wq_w[:, e, cols].bitcast(FP8X4), lhsT_scale=wq_s[FIRST_ROW["wq"] :, e, cols],
+                sums = psum.tile([P, C], F32, name="sums%d" % b)
+                nc.tensor.matmul_mx(out=sums[:], lhsT=wq_w[:, e, cols].bitcast(FP8X4), lhsT_scale=wq_s[FIRST_ROW["wq"] :, e, cols],
                                     rhs=q_w[:, slots].bitcast(FP8X4), rhs_scale=q_s[FIRST_ROW["q"] :, slots], start=True, stop=False)
                 for h in range(C // P):
                     half = slice(e * C + h * P, e * C + (h + 1) * P)
-                    nc.tensor.matmul_mx(out=sums[b][:, h * P : (h + 1) * P], lhsT=wv_w[:, e, 2 * b * P : 2 * (b + 1) * P].bitcast(FP4X4),
+                    nc.tensor.matmul_mx(out=sums[:, h * P : (h + 1) * P], lhsT=wv_w[:, e, 2 * b * P : 2 * (b + 1) * P].bitcast(FP4X4),
                                         lhsT_scale=wv_s[:, e, cols], rhs=v_w[:, half].bitcast(FP8X4), rhs_scale=v_s[:, half],
                                         start=False, stop=False)
-                nc.tensor.matmul_mx(out=sums[b][:], lhsT=wk_w[e][:, cols].bitcast(FP8X4), lhsT_scale=wk_s[e][:, cols],
+                nc.tensor.matmul_mx(out=sums[:], lhsT=wk_w[e][:, cols].bitcast(FP8X4), lhsT_scale=wk_s[e][:, cols],
                                     rhs=k_w[e][:].bitcast(FP8X4), rhs_scale=k_s[e][FIRST_ROW["k"] :, :], start=False, stop=True)
-            for b in range(BLOCKS):
                 dx = tile([P, C], F32, "dx%d_%d" % (e, b))
-                nc.scalar.copy(out=dx[:], in_=sums[b][:])
-                nc.vector.tensor_tensor(result[b][:].indirect(offsets[:, e * LIST_COLS : (e + 1) * LIST_COLS]), dx[:], gates[:, slots], MULT)
+                nc.scalar.copy(out=dx[:], in_=sums[:])
+                nc.vector.tensor_tensor(result[b][:].indirect(offsets[:, e * LIST_COLS : (e + 1) * LIST_COLS]), dx[:], gates[e][:], MULT)
+                if e == 0 and b == 0:
+                    quantize_wk(1)
 
         for b in range(BLOCKS):
-            nc.sync.dma_start(out=out[b * P : (b + 1) * P, :], in_=result[b][:])
+            nc.sync.dma_start(out=out[b * P : (b + 1) * P, :], in_=result[b][:, 0:T])

@@ -46,7 +46,7 @@ def tile_moe_qkb_kernel(tc, dq_words, dq_scales, dk_words, dk_scales, dv_words, 
         result = [tile([P, T], F32, "result0"), tile([P, T + K * PACK // 2], F32, "result1")]
         wk_bf = [tile([P, K * PACK], BF16, "wk_bf0")[:], result[1][:, T:].bitcast(BF16)]
 
-        for g in "qvk":
+        for g in "vk":
             nc.vector.memset(table_s[g][:].bitcast(I32), 0)
         zero = tile([P, 8], F32, "zero")
         nc.vector.memset(zero[:], 0.0)
@@ -56,9 +56,9 @@ def tile_moe_qkb_kernel(tc, dq_words, dq_scales, dk_words, dk_scales, dv_words, 
         def load_table_words(queue, g, words):
             queue.dma_start(out=table_w[g][:].bitcast(I32), in_=words[0].rearrange("p t d -> p (t d)").bitcast(I32))
 
-        def load_table_scales(queue, g, scales):
+        def load_table_scales(queue, g, scales, which=range(4)):
             rows = scales[0].rearrange("(q r) t -> r q t", r=4)
-            for r in range(4):
+            for r in which:
                 queue.dma_start(out=table_s[g][FIRST_ROW[g] + r : P : QUAD, :].bitcast(I32), in_=rows[r].bitcast(I32))
 
         def load_weight_scales(queue, plane, scales, first):
@@ -70,15 +70,18 @@ def tile_moe_qkb_kernel(tc, dq_words, dq_scales, dk_words, dk_scales, dv_words, 
             queue.dma_start(out=wk_raw[e][:], in_=wk[e].rearrange("(p j) c -> p j c", j=PACK))
 
         nc.sync.dma_start(offsets[:], offs)
+        for q in range(P // QUAD):
+            rows = dq_scales[0, 4 * q : 4 * q + 4, :].bitcast(I32)
+            nc.sync.dma_start(out=table_s["q"][q * QUAD : (q + 1) * QUAD, :].bitcast(I32), in_=rows.unsqueeze(0).to_broadcast([QUAD // 4, 4, T // 4]))
         load_table_words(nc.sync, "q", dq_words)
-        load_table_scales(nc.sync, "q", dq_scales)
         load_table_words(nc.sync, "v", dv_words)
-        load_wk(nc.sync, 0)
         load_table_scales(nc.sync, "v", dv_scales)
-        load_table_words(nc.sync, "k", dk_words)
-        load_table_scales(nc.sync, "k", dk_scales)
-        load_weight_scales(nc.gpsimd, wq_s, wq_scales, FIRST_ROW["wq"])
+        load_wk(nc.sync, 0)
+        load_table_scales(nc.sync, "k", dk_scales, range(0, 2))
         nc.sync.dma_start(out=wq_w[:].bitcast(I32), in_=wq_words.rearrange("e s p c d -> p (e s) (c d)").bitcast(I32))
+        load_table_scales(nc.sync, "k", dk_scales, range(2, 4))
+        load_table_words(nc.sync, "k", dk_words)
+        load_weight_scales(nc.gpsimd, wq_s, wq_scales, FIRST_ROW["wq"])
         nc.sync.dma_start(out=wv_w[:].bitcast(I32), in_=wv_words.rearrange("e s p b -> p (e s) b").bitcast(I32))
         load_weight_scales(nc.sync, wv_s, wv_scales, FIRST_ROW["wv"])
         nc.sync.dma_start(out=gates[0][:], in_=gate[:, 0:C])
@@ -97,16 +100,16 @@ def tile_moe_qkb_kernel(tc, dq_words, dq_scales, dk_words, dk_scales, dv_words, 
             )
             nc.vector.quantize_mx(out=wk_w[e][:].bitcast(FP8X4), scales=wk_s[e][:], in_=wk_bf[e])
 
-        q_w = gather(table_w["q"], U32, "q_w", 0, E)
         q_s = gather(table_s["q"], U8, "q_s", 0, E)
+        q_w = gather(table_w["q"], U32, "q_w", 0, E)
         v_w = gather(table_w["v"], U32, "v_w", 0, E)
         v_s = gather(table_s["v"], U8, "v_s", 0, E)
-        quantize_wk(0)
         k_w, k_s = [], []
-        k_w.append(gather(table_w["k"], U32, "k_w0", 0, 1))
         k_s.append(gather(table_s["k"], U8, "k_s0", 0, 1))
-        k_s.append(gather(table_s["k"], U8, "k_s1", 1, 2))
-        k_w.append(gather(table_w["k"], U32, "table_s_k", 1, 2))
+        quantize_wk(0)
+        k_w.append(gather(table_w["k"], U32, "k_w0", 0, 1))
+        k_w.append(gather(table_w["k"], U32, "k_w1", 1, 2))
+        k_s.append(gather(table_s["k"], U8, "table_w_k", 1, 2))
 
         for e in range(E):
             slots = slice(e * C, (e + 1) * C)

@@ -72,7 +72,8 @@ def tile_moe_qkb_kernel(tc, dq_words, dq_scales, dk_words, dk_scales, dv_words, 
         nc.sync.dma_start(offsets[:], offs)
         for q in range(P // QUAD):
             rows = dq_scales[0, 4 * q : 4 * q + 4, :].bitcast(I32)
-            nc.sync.dma_start(out=table_s["q"][q * QUAD : (q + 1) * QUAD, :].bitcast(I32), in_=rows.unsqueeze(0).to_broadcast([QUAD // 4, 4, T // 4]))
+            queue = nc.sync if q < 2 else nc.scalar
+            queue.dma_start(out=table_s["q"][q * QUAD : (q + 1) * QUAD, :].bitcast(I32), in_=rows.unsqueeze(0).to_broadcast([QUAD // 4, 4, T // 4]))
         load_table_words(nc.sync, "q", dq_words)
         load_table_words(nc.sync, "v", dv_words)
         load_table_scales(nc.sync, "v", dv_scales)

@@ -69,11 +69,11 @@ def tile_moe_qkb_kernel(tc, dq_words, dq_scales, dk_words, dk_scales, dv_words, 
         def load_wk(queue, e):
             queue.dma_start(out=wk_raw[e][:], in_=wk[e].rearrange("(p j) c -> p j c", j=PACK))
 
-        nc.sync.dma_start(offsets[:], offs)
         for q in range(P // QUAD):
             rows = dq_scales[0, 4 * q : 4 * q + 4, :].bitcast(I32)
             queue = nc.sync if q < 2 else nc.scalar
             queue.dma_start(out=table_s["q"][q * QUAD : (q + 1) * QUAD, :].bitcast(I32), in_=rows.unsqueeze(0).to_broadcast([QUAD // 4, 4, T // 4]))
+        nc.sync.dma_start(offsets[:], offs)
         load_table_words(nc.sync, "q", dq_words)
         load_table_words(nc.sync, "v", dv_words)
         load_table_scales(nc.sync, "v", dv_scales)

@@ -43,8 +43,8 @@ def tile_moe_qkb_kernel(tc, dq_words, dq_scales, dk_words, dk_scales, dv_words, 
         wk_w = [tile([P, K], U32, "wk_w%d" % e) for e in range(E)]
         wk_s = [tile([P, K], U8, "wk_s%d" % e) for e in range(E)]
         gates = [tile([P, C], F32, "gates%d" % e) for e in range(E)]
-        result = [tile([P, T], F32, "result0"), tile([P, T + K * PACK // 2], F32, "result1")]
-        wk_bf = [tile([P, K * PACK], BF16, "wk_bf0")[:], result[1][:, T:].bitcast(BF16)]
+        result = [tile([P, T], F32, "result%d" % b) for b in range(BLOCKS)]
+        wk_bf = [tile([P, K * PACK], BF16, "wk_bf%d" % e)[:] for e in range(E)]
 
         for g in "vk":
             nc.vector.memset(table_s[g][:].bitcast(I32), 0)
@@ -126,7 +126,7 @@ def tile_moe_qkb_kernel(tc, dq_words, dq_scales, dk_words, dk_scales, dv_words, 
                                         start=False, stop=False)
                 nc.tensor.matmul_mx(out=sums[:], lhsT=wk_w[e][:, cols].bitcast(FP8X4), lhsT_scale=wk_s[e][:, cols],
                                     rhs=k_w[e][:].bitcast(FP8X4), rhs_scale=k_s[e][FIRST_ROW["k"] :, :], start=False, stop=True)
-                dx = tile([P, C], F32, "dx%d_%d" % (e, b))
+                dx = tile([P, C], F32, "wk_raw1" if (e, b) == (0, 1) else "dx%d_%d" % (e, b))
                 nc.scalar.copy(out=dx[:], in_=sums[:])
                 nc.vector.tensor_tensor(result[b][:].indirect(offsets[:, e * LIST_COLS : (e + 1) * LIST_COLS]), dx[:], gates[e][:], MULT)
                 if e == 0 and b == 0:

@@ -18,7 +18,7 @@ MULT = mybir.AluOpType.mult
 P = 128
 PACK = 4
 QUAD = 32
-BLOCKS = K // P
+BANDS = K // P
 LIST_COLS = C // 16
 FIRST_ROW = {"q": 4, "k": 12, "v": 0, "wq": 8, "wv": 0}
 
@@ -40,97 +40,103 @@ def tile_moe_qkb_kernel(tc, dq_words, dq_scales, dk_words, dk_scales, dv_words, 
         wv_w = tile([P, E, 2 * K], U8, "wv_w")
         wv_s = tile([P, E, K], U8, "wv_s")
         wk_raw = [tile([P, PACK, K], F32, "wk_raw%d" % e) for e in range(E)]
-        wk_w = [tile([P, K], U32, "wk_w%d" % e) for e in range(E)]
-        wk_s = [tile([P, K], U8, "wk_s%d" % e) for e in range(E)]
-        gates = [tile([P, C], F32, "gates%d" % e) for e in range(E)]
-        result = [tile([P, T], F32, "result%d" % b) for b in range(BLOCKS)]
-        wk_bf = [tile([P, K * PACK], BF16, "wk_bf%d" % e)[:] for e in range(E)]
+        wk_bf = [tile([P, K * PACK], BF16, "wk_bf%d" % e) for e in range(E)]
+        gates = tile([P, E * C], F32, "gates")
+        result = [tile([P, T], F32, "result%d" % b) for b in range(BANDS)]
 
         for g in "vk":
             nc.vector.memset(table_s[g][:].bitcast(I32), 0)
         zero = tile([P, 8], F32, "zero")
         nc.vector.memset(zero[:], 0.0)
-        for b in range(BLOCKS):
-            nc.scalar.copy(out=result[b][:, 0:T], in_=zero[:, 0:1].to_broadcast([P, T]))
+        for b in range(BANDS):
+            nc.scalar.copy(out=result[b][:], in_=zero[:, 0:1].to_broadcast([P, T]))
 
-        def load_table_words(queue, g, words):
-            queue.dma_start(out=table_w[g][:].bitcast(I32), in_=words[0].rearrange("p t d -> p (t d)").bitcast(I32))
+        def load_table_words(g, words):
+            nc.sync.dma_start(out=table_w[g][:].bitcast(I32), in_=words[0].rearrange("p t d -> p (t d)").bitcast(I32))
 
-        def load_table_scales(queue, g, scales, which=range(4)):
+        def load_table_scales(g, scales, which):
             rows = scales[0].rearrange("(q r) t -> r q t", r=4)
             for r in which:
-                queue.dma_start(out=table_s[g][FIRST_ROW[g] + r : P : QUAD, :].bitcast(I32), in_=rows[r].bitcast(I32))
+                nc.sync.dma_start(out=table_s[g][FIRST_ROW[g] + r : P : QUAD, :].bitcast(I32), in_=rows[r].bitcast(I32))
 
-        def load_weight_scales(queue, plane, scales, first):
+        def load_weight_scales(queue, plane, scales, first, which=range(4)):
             rows = scales.rearrange("e s (q r) c -> r q (e s) c", r=4)
-            for r in range(4):
+            for r in which:
                 queue.dma_start(out=plane[first + r : P : QUAD, :, :].bitcast(I32), in_=rows[r].bitcast(I32))
 
-        def load_wk(queue, e):
-            queue.dma_start(out=wk_raw[e][:], in_=wk[e].rearrange("(p j) c -> p j c", j=PACK))
+        def load_wk(e):
+            nc.sync.dma_start(out=wk_raw[e][:], in_=wk[e].rearrange("(p j) c -> p j c", j=PACK))
 
         for q in range(P // QUAD):
             rows = dq_scales[0, 4 * q : 4 * q + 4, :].bitcast(I32)
             queue = nc.sync if q < 2 else nc.scalar
             queue.dma_start(out=table_s["q"][q * QUAD : (q + 1) * QUAD, :].bitcast(I32), in_=rows.unsqueeze(0).to_broadcast([QUAD // 4, 4, T // 4]))
         nc.sync.dma_start(offsets[:], offs)
-        load_table_words(nc.sync, "q", dq_words)
-        load_table_words(nc.sync, "v", dv_words)
-        load_table_scales(nc.sync, "v", dv_scales)
-        load_wk(nc.sync, 0)
-        load_table_scales(nc.sync, "k", dk_scales, range(0, 2))
-        nc.sync.dma_start(out=wq_w[:].bitcast(I32), in_=wq_words.rearrange("e s p c d -> p (e s) (c d)").bitcast(I32))
-        load_table_scales(nc.sync, "k", dk_scales, range(2, 4))
-        load_table_words(nc.sync, "k", dk_words)
         load_weight_scales(nc.gpsimd, wq_s, wq_scales, FIRST_ROW["wq"])
+        load_table_words("q", dq_words)
+        load_table_words("v", dv_words)
+        load_table_scales("v", dv_scales, range(0, 4))
+        load_wk(0)
+        load_table_scales("k", dk_scales, range(0, 2))
+        nc.sync.dma_start(out=wq_w[:].bitcast(I32), in_=wq_words.rearrange("e s p c d -> p (e s) (c d)").bitcast(I32))
+        load_table_scales("k", dk_scales, range(2, 4))
+        load_table_words("k", dk_words)
         nc.sync.dma_start(out=wv_w[:].bitcast(I32), in_=wv_words.rearrange("e s p b -> p (e s) b").bitcast(I32))
-        load_weight_scales(nc.sync, wv_s, wv_scales, FIRST_ROW["wv"])
-        nc.sync.dma_start(out=gates[0][:], in_=gate[:, 0:C])
-        load_wk(nc.sync, 1)
-        nc.sync.dma_start(out=gates[1][:], in_=gate[:, C : 2 * C])
+        load_weight_scales(nc.sync, wv_s, wv_scales, FIRST_ROW["wv"], range(0, 4))
+        nc.sync.dma_start(out=gates[:, 0:C], in_=gate[:, 0:C])
+        load_wk(1)
+        nc.sync.dma_start(out=gates[:, C : 2 * C], in_=gate[:, C : 2 * C])
 
         def gather(table, dtype, name, lo, hi):
             slots = tile([P, (hi - lo) * C], dtype, name)
             nc.vector.tensor_copy(slots[:], table[:].indirect(offsets[:, lo * LIST_COLS : hi * LIST_COLS]))
             return slots
 
-        def quantize_wk(e):
-            nc.scalar.copy(
-                out=wk_bf[e].rearrange("p (c i j) -> p c j i", i=4, j=PACK),
-                in_=wk_raw[e][:].rearrange("p j (c i) -> p c j i", i=4),
-            )
-            nc.vector.quantize_mx(out=wk_w[e][:].bitcast(FP8X4), scales=wk_s[e][:], in_=wk_bf[e])
+        wk_w, wk_s = {}, {}
+
+        def quantize_wk(e, lo, hi):
+            cols = slice(lo * P, hi * P)
+            rounded = wk_bf[e][:, PACK * lo * P : PACK * hi * P]
+            nc.scalar.copy(out=rounded.rearrange("p (c i j) -> p c j i", i=4, j=PACK), in_=wk_raw[e][:, :, cols].rearrange("p j (c i) -> p c j i", i=4))
+            codes = tile([P, (hi - lo) * P], U32, "wk_w%d_%d" % (e, lo))
+            plane = tile([P, (hi - lo) * P], U8, "wk_s%d_%d" % (e, lo))
+            nc.vector.quantize_mx(out=codes[:].bitcast(FP8X4), scales=plane[:], in_=rounded)
+            for b in range(lo, hi):
+                wk_w[e, b] = codes[:, (b - lo) * P : (b - lo + 1) * P]
+                wk_s[e, b] = plane[:, (b - lo) * P : (b - lo + 1) * P]
 
         q_s = gather(table_s["q"], U8, "q_s", 0, E)
         q_w = gather(table_w["q"], U32, "q_w", 0, E)
         v_w = gather(table_w["v"], U32, "v_w", 0, E)
         v_s = gather(table_s["v"], U8, "v_s", 0, E)
-        k_w, k_s = [], []
-        k_s.append(gather(table_s["k"], U8, "k_s0", 0, 1))
-        quantize_wk(0)
-        k_w.append(gather(table_w["k"], U32, "k_w0", 0, 1))
-        k_w.append(gather(table_w["k"], U32, "k_w1", 1, 2))
-        k_s.append(gather(table_s["k"], U8, "table_w_k", 1, 2))
+        k_s = [gather(table_s["k"], U8, "k_s0", 0, 1)]
+        for b in range(BANDS):
+            quantize_wk(0, b, b + 1)
+        k_w = [gather(table_w["k"], U32, "k_w%d" % e, e, e + 1) for e in range(E)]
+
+        def products(e, b, bank):
+            slots = slice(e * C, (e + 1) * C)
+            cols = slice(b * P, (b + 1) * P)
+            sums = psum.tile([P, C], F32, name="sums%d" % bank)
+            nc.tensor.matmul_mx(out=sums[:], lhsT=wq_w[:, e, cols].bitcast(FP8X4), lhsT_scale=wq_s[FIRST_ROW["wq"] :, e, cols],
+                                rhs=q_w[:, slots].bitcast(FP8X4), rhs_scale=q_s[FIRST_ROW["q"] :, slots], start=True, stop=False)
+            for h in range(C // P):
+                half = slice(e * C + h * P, e * C + (h + 1) * P)
+                nc.tensor.matmul_mx(out=sums[:, h * P : (h + 1) * P], lhsT=wv_w[:, e, 2 * b * P : 2 * (b + 1) * P].bitcast(FP4X4),
+                                    lhsT_scale=wv_s[:, e, cols], rhs=v_w[:, half].bitcast(FP8X4), rhs_scale=v_s[:, half],
+                                    start=False, stop=False)
+            nc.tensor.matmul_mx(out=sums[:], lhsT=wk_w[e, b].bitcast(FP8X4), lhsT_scale=wk_s[e, b],
+                                rhs=k_w[e][:].bitcast(FP8X4), rhs_scale=k_s[e][FIRST_ROW["k"] :, :], start=False, stop=True)
+            if (e, b) == (0, 0):
+                k_s.append(gather(table_s["k"], U8, "wk_s0_0", 1, 2))
+            dx = tile([P, C], F32, "wk_raw1" if (e, b) == (0, 1) else "dx%d_%d" % (e, b))
+            nc.scalar.copy(out=dx[:], in_=sums[:])
+            nc.vector.tensor_tensor(result[b][:].indirect(offsets[:, e * LIST_COLS : (e + 1) * LIST_COLS]), dx[:], gates[:, slots], MULT)
 
         for e in range(E):
-            slots = slice(e * C, (e + 1) * C)
-            for b in range(BLOCKS):
-                cols = slice(b * P, (b + 1) * P)
-                sums = psum.tile([P, C], F32, name="sums%d" % b)
-                nc.tensor.matmul_mx(out=sums[:], lhsT=wq_w[:, e, cols].bitcast(FP8X4), lhsT_scale=wq_s[FIRST_ROW["wq"] :, e, cols],
-                                    rhs=q_w[:, slots].bitcast(FP8X4), rhs_scale=q_s[FIRST_ROW["q"] :, slots], start=True, stop=False)
-                for h in range(C // P):
-                    half = slice(e * C + h * P, e * C + (h + 1) * P)
-                    nc.tensor.matmul_mx(out=sums[:, h * P : (h + 1) * P], lhsT=wv_w[:, e, 2 * b * P : 2 * (b + 1) * P].bitcast(FP4X4),
-                                        lhsT_scale=wv_s[:, e, cols], rhs=v_w[:, half].bitcast(FP8X4), rhs_scale=v_s[:, half],
-                                        start=False, stop=False)
-                nc.tensor.matmul_mx(out=sums[:], lhsT=wk_w[e][:, cols].bitcast(FP8X4), lhsT_scale=wk_s[e][:, cols],
-                                    rhs=k_w[e][:].bitcast(FP8X4), rhs_scale=k_s[e][FIRST_ROW["k"] :, :], start=False, stop=True)
-                dx = tile([P, C], F32, "wk_raw1" if (e, b) == (0, 1) else "dx%d_%d" % (e, b))
-                nc.scalar.copy(out=dx[:], in_=sums[:])
-                nc.vector.tensor_tensor(result[b][:].indirect(offsets[:, e * LIST_COLS : (e + 1) * LIST_COLS]), dx[:], gates[e][:], MULT)
-                if e == 0 and b == 0:
-                    quantize_wk(1)
-
-        for b in range(BLOCKS):
-            nc.sync.dma_start(out=out[b * P : (b + 1) * P, :], in_=result[b][:, 0:T])
+            for b in range(BANDS):
+                products(e, b, b)
+                if (e, b) == (0, 0):
+                    quantize_wk(1, 0, BANDS)
+        for b in range(BANDS):
+            nc.sync.dma_start(out=out[b * P : (b + 1) * P, :], in_=result[b][:])

@@ -35,9 +35,9 @@ def tile_moe_qkb_kernel(tc, dq_words, dq_scales, dk_words, dk_scales, dv_words, 
         offsets = keep.tile([P, E * LIST_COLS], U16, name="offsets")
         table_w = {g: tile([P, T], U32, "table_w_" + g) for g in "qkv"}
         table_s = {g: tile([P, T], U8, "table_s_" + g) for g in "qkv"}
-        wq_w = tile([P, E, K], U32, "wq_w")
+        wq_w = [tile([P, K], U32, "wq_w%d" % e) for e in range(E)]
         wq_s = tile([P, E, K], U8, "wq_s")
-        wv_w = tile([P, E, 2 * K], U8, "wv_w")
+        wv_w = [tile([P, 2 * K], U8, "wv_w%d" % e) for e in range(E)]
         wv_s = tile([P, E, K], U8, "wv_s")
         wk_raw = [tile([P, PACK, K], F32, "wk_raw%d" % e) for e in range(E)]
         wk_bf = [tile([P, K * PACK], BF16, "wk_bf%d" % e) for e in range(E)]
@@ -78,13 +78,15 @@ def tile_moe_qkb_kernel(tc, dq_words, dq_scales, dk_words, dk_scales, dv_words, 
         load_table_scales("v", dv_scales, range(0, 4))
         load_wk(0)
         load_table_scales("k", dk_scales, range(0, 2))
-        nc.sync.dma_start(out=wq_w[:].bitcast(I32), in_=wq_words.rearrange("e s p c d -> p (e s) (c d)").bitcast(I32))
+        nc.sync.dma_start(out=wq_w[0][:].bitcast(I32), in_=wq_words[0, 0].rearrange("p c d -> p (c d)").bitcast(I32))
         load_table_scales("k", dk_scales, range(2, 4))
         load_table_words("k", dk_words)
-        nc.sync.dma_start(out=wv_w[:].bitcast(I32), in_=wv_words.rearrange("e s p b -> p (e s) b").bitcast(I32))
+        nc.sync.dma_start(out=wv_w[0][:].bitcast(I32), in_=wv_words[0, 0].bitcast(I32))
         load_weight_scales(nc.sync, wv_s, wv_scales, FIRST_ROW["wv"], range(0, 4))
         nc.sync.dma_start(out=gates[:, 0:C], in_=gate[:, 0:C])
         load_wk(1)
+        nc.sync.dma_start(out=wq_w[1][:].bitcast(I32), in_=wq_words[1, 0].rearrange("p c d -> p (c d)").bitcast(I32))
+        nc.sync.dma_start(out=wv_w[1][:].bitcast(I32), in_=wv_words[1, 0].bitcast(I32))
         nc.sync.dma_start(out=gates[:, C : 2 * C], in_=gate[:, C : 2 * C])
 
         def gather(table, dtype, name, lo, hi):
@@ -118,11 +120,11 @@ def tile_moe_qkb_kernel(tc, dq_words, dq_scales, dk_words, dk_scales, dv_words, 
             slots = slice(e * C, (e + 1) * C)
             cols = slice(b * P, (b + 1) * P)
             sums = psum.tile([P, C], F32, name="sums%d" % bank)
-            nc.tensor.matmul_mx(out=sums[:], lhsT=wq_w[:, e, cols].bitcast(FP8X4), lhsT_scale=wq_s[FIRST_ROW["wq"] :, e, cols],
+            nc.tensor.matmul_mx(out=sums[:], lhsT=wq_w[e][:, cols].bitcast(FP8X4), lhsT_scale=wq_s[FIRST_ROW["wq"] :, e, cols],
                                 rhs=q_w[:, slots].bitcast(FP8X4), rhs_scale=q_s[FIRST_ROW["q"] :, slots], start=True, stop=False)
             for h in range(C // P):
                 half = slice(e * C + h * P, e * C + (h + 1) * P)
-                nc.tensor.matmul_mx(out=sums[:, h * P : (h + 1) * P], lhsT=wv_w[:, e, 2 * b * P : 2 * (b + 1) * P].bitcast(FP4X4),
+                nc.tensor.matmul_mx(out=sums[:, h * P : (h + 1) * P], lhsT=wv_w[e][:, 2 * b * P : 2 * (b + 1) * P].bitcast(FP4X4),
                                     lhsT_scale=wv_s[:, e, cols], rhs=v_w[:, half].bitcast(FP8X4), rhs_scale=v_s[:, half],
                                     start=False, stop=False)
             nc.tensor.matmul_mx(out=sums[:], lhsT=wk_w[e, b].bitcast(FP8X4), lhsT_scale=wk_s[e, b],

@@ -37,10 +37,14 @@ def tile_moe_qkb_kernel(tc, dq_words, dq_scales, dk_words, dk_scales, dv_words, 
         table_s = {g: tile([P, T], U8, "table_s_" + g) for g in "qkv"}
         wq_w = [tile([P, K], U32, "wq_w%d" % e) for e in range(E)]
         wq_s = tile([P, E, K], U8, "wq_s")
-        wv_w = [tile([P, 2 * K], U8, "wv_w%d" % e) for e in range(E)]
+        wv_first = [tile([P, 2 * P], U8, "wv_first%d" % b) for b in range(BANDS)]
+        wv_second = tile([P, 2 * K], U8, "wv_second")
+        wv_w = {(e, b): wv_second[:, 2 * b * P : 2 * (b + 1) * P] if e else wv_first[b][:] for e in range(E) for b in range(BANDS)}
         wv_s = tile([P, E, K], U8, "wv_s")
         wk_raw = [tile([P, PACK, K], F32, "wk_raw%d" % e) for e in range(E)]
         wk_bf = [tile([P, K * PACK], BF16, "wk_bf%d" % e) for e in range(E)]
+        wk_w = [tile([P, K], U32, "wk_w%d" % e) for e in range(E)]
+        wk_s = [tile([P, K], U8, "wk_s%d" % e) for e in range(E)]
         gates = tile([P, E * C], F32, "gates")
         result = [tile([P, T], F32, "result%d" % b) for b in range(BANDS)]
 
@@ -81,12 +85,13 @@ def tile_moe_qkb_kernel(tc, dq_words, dq_scales, dk_words, dk_scales, dv_words, 
         nc.sync.dma_start(out=wq_w[0][:].bitcast(I32), in_=wq_words[0, 0].rearrange("p c d -> p (c d)").bitcast(I32))
         load_table_scales("k", dk_scales, range(2, 4))
         load_table_words("k", dk_words)
-        nc.sync.dma_start(out=wv_w[0][:].bitcast(I32), in_=wv_words[0, 0].bitcast(I32))
+        nc.sync.dma_start(out=wv_first[0][:].bitcast(I32), in_=wv_words[0, 0, :, 0 * P : 2 * P].bitcast(I32))
         load_weight_scales(nc.sync, wv_s, wv_scales, FIRST_ROW["wv"], range(0, 4))
         nc.sync.dma_start(out=gates[:, 0:C], in_=gate[:, 0:C])
         load_wk(1)
+        nc.sync.dma_start(out=wv_first[1][:].bitcast(I32), in_=wv_words[0, 0, :, 2 * P : 4 * P].bitcast(I32))
         nc.sync.dma_start(out=wq_w[1][:].bitcast(I32), in_=wq_words[1, 0].rearrange("p c d -> p (c d)").bitcast(I32))
-        nc.sync.dma_start(out=wv_w[1][:].bitcast(I32), in_=wv_words[1, 0].bitcast(I32))
+        nc.sync.dma_start(out=wv_second[:].bitcast(I32), in_=wv_words[1, 0].bitcast(I32))
         nc.sync.dma_start(out=gates[:, C : 2 * C], in_=gate[:, C : 2 * C])
 
         def gather(table, dtype, name, lo, hi):
@@ -94,26 +99,19 @@ def tile_moe_qkb_kernel(tc, dq_words, dq_scales, dk_words, dk_scales, dv_words, 
             nc.vector.tensor_copy(slots[:], table[:].indirect(offsets[:, lo * LIST_COLS : hi * LIST_COLS]))
             return slots
 
-        wk_w, wk_s = {}, {}
-
-        def quantize_wk(e, lo, hi):
-            cols = slice(lo * P, hi * P)
-            rounded = wk_bf[e][:, PACK * lo * P : PACK * hi * P]
-            nc.scalar.copy(out=rounded.rearrange("p (c i j) -> p c j i", i=4, j=PACK), in_=wk_raw[e][:, :, cols].rearrange("p j (c i) -> p c j i", i=4))
-            codes = tile([P, (hi - lo) * P], U32, "wk_w%d_%d" % (e, lo))
-            plane = tile([P, (hi - lo) * P], U8, "wk_s%d_%d" % (e, lo))
-            nc.vector.quantize_mx(out=codes[:].bitcast(FP8X4), scales=plane[:], in_=rounded)
-            for b in range(lo, hi):
-                wk_w[e, b] = codes[:, (b - lo) * P : (b - lo + 1) * P]
-                wk_s[e, b] = plane[:, (b - lo) * P : (b - lo + 1) * P]
+        def quantize_wk(e):
+            nc.scalar.copy(
+                out=wk_bf[e][:].rearrange("p (c i j) -> p c j i", i=4, j=PACK),
+                in_=wk_raw[e][:].rearrange("p j (c i) -> p c j i", i=4),
+            )
+            nc.vector.quantize_mx(out=wk_w[e][:].bitcast(FP8X4), scales=wk_s[e][:], in_=wk_bf[e][:])
 
         q_s = gather(table_s["q"], U8, "q_s", 0, E)
         q_w = gather(table_w["q"], U32, "q_w", 0, E)
         v_w = gather(table_w["v"], U32, "v_w", 0, E)
         v_s = gather(table_s["v"], U8, "v_s", 0, E)
         k_s = [gather(table_s["k"], U8, "k_s0", 0, 1)]
-        for b in range(BANDS):
-            quantize_wk(0, b, b + 1)
+        quantize_wk(0)
         k_w = [gather(table_w["k"], U32, "k_w%d" % e, e, e + 1) for e in range(E)]
 
         def products(e, b, bank):
@@ -124,13 +122,13 @@ def tile_moe_qkb_kernel(tc, dq_words, dq_scales, dk_words, dk_scales, dv_words, 
                                 rhs=q_w[:, slots].bitcast(FP8X4), rhs_scale=q_s[FIRST_ROW["q"] :, slots], start=True, stop=False)
             for h in range(C // P):
                 half = slice(e * C + h * P, e * C + (h + 1) * P)
-                nc.tensor.matmul_mx(out=sums[:, h * P : (h + 1) * P], lhsT=wv_w[e][:, 2 * b * P : 2 * (b + 1) * P].bitcast(FP4X4),
+                nc.tensor.matmul_mx(out=sums[:, h * P : (h + 1) * P], lhsT=wv_w[e, b].bitcast(FP4X4),
                                     lhsT_scale=wv_s[:, e, cols], rhs=v_w[:, half].bitcast(FP8X4), rhs_scale=v_s[:, half],
                                     start=False, stop=False)
-            nc.tensor.matmul_mx(out=sums[:], lhsT=wk_w[e, b].bitcast(FP8X4), lhsT_scale=wk_s[e, b],
-                                rhs=k_w[e][:].bitcast(FP8X4), rhs_scale=k_s[e][FIRST_ROW["k"] :, :], start=False, stop=True)
             if (e, b) == (0, 0):
-                k_s.append(gather(table_s["k"], U8, "wk_s0_0", 1, 2))
+                k_s.append(gather(table_s["k"], U8, "wv_first0", 1, 2))
+            nc.tensor.matmul_mx(out=sums[:], lhsT=wk_w[e][:, cols].bitcast(FP8X4), lhsT_scale=wk_s[e][:, cols],
+                                rhs=k_w[e][:].bitcast(FP8X4), rhs_scale=k_s[e][FIRST_ROW["k"] :, :], start=False, stop=True)
             dx = tile([P, C], F32, "wk_raw1" if (e, b) == (0, 1) else "dx%d_%d" % (e, b))
             nc.scalar.copy(out=dx[:], in_=sums[:])
             nc.vector.tensor_tensor(result[b][:].indirect(offsets[:, e * LIST_COLS : (e + 1) * LIST_COLS]), dx[:], gates[:, slots], MULT)
@@ -139,6 +137,6 @@ def tile_moe_qkb_kernel(tc, dq_words, dq_scales, dk_words, dk_scales, dv_words, 
             for b in range(BANDS):
                 products(e, b, b)
                 if (e, b) == (0, 0):
-                    quantize_wk(1, 0, BANDS)
+                    quantize_wk(1)
         for b in range(BANDS):
             nc.sync.dma_start(out=out[b * P : (b + 1) * P, :], in_=result[b][:])

@@ -35,11 +35,12 @@ def tile_moe_qkb_kernel(tc, dq_words, dq_scales, dk_words, dk_scales, dv_words, 
         offsets = keep.tile([P, E * LIST_COLS], U16, name="offsets")
         table_w = {g: tile([P, T], U32, "table_w_" + g) for g in "qkv"}
         table_s = {g: tile([P, T], U8, "table_s_" + g) for g in "qkv"}
-        wq_w = [tile([P, K], U32, "wq_w%d" % e) for e in range(E)]
+        wq_first = [tile([P, P], U32, "wq_first%d" % b) for b in range(BANDS)]
+        wq_second = tile([P, K], U32, "wq_second")
+        wq_w = {(e, b): wq_second[:, b * P : (b + 1) * P] if e else wq_first[b][:] for e in range(E) for b in range(BANDS)}
         wq_s = tile([P, E, K], U8, "wq_s")
-        wv_first = [tile([P, 2 * P], U8, "wv_first%d" % b) for b in range(BANDS)]
-        wv_second = tile([P, 2 * K], U8, "wv_second")
-        wv_w = {(e, b): wv_second[:, 2 * b * P : 2 * (b + 1) * P] if e else wv_first[b][:] for e in range(E) for b in range(BANDS)}
+        wv_all = [tile([P, 2 * K], U8, "wv_w%d" % e) for e in range(E)]
+        wv_w = {(e, b): wv_all[e][:, 2 * b * P : 2 * (b + 1) * P] for e in range(E) for b in range(BANDS)}
         wv_s = tile([P, E, K], U8, "wv_s")
         wk_raw = [tile([P, PACK, K], F32, "wk_raw%d" % e) for e in range(E)]
         wk_bf = [tile([P, K * PACK], BF16, "wk_bf%d" % e) for e in range(E)]
@@ -48,7 +49,7 @@ def tile_moe_qkb_kernel(tc, dq_words, dq_scales, dk_words, dk_scales, dv_words, 
         gates = tile([P, E * C], F32, "gates")
         result = [tile([P, T], F32, "result%d" % b) for b in range(BANDS)]
 
-        for g in "vk":
+        for g in "kv":
             nc.vector.memset(table_s[g][:].bitcast(I32), 0)
         zero = tile([P, 8], F32, "zero")
         nc.vector.memset(zero[:], 0.0)
@@ -78,20 +79,20 @@ def tile_moe_qkb_kernel(tc, dq_words, dq_scales, dk_words, dk_scales, dv_words, 
         nc.sync.dma_start(offsets[:], offs)
         load_weight_scales(nc.gpsimd, wq_s, wq_scales, FIRST_ROW["wq"])
         load_table_words("q", dq_words)
-        load_table_words("v", dv_words)
-        load_table_scales("v", dv_scales, range(0, 4))
-        load_wk(0)
-        load_table_scales("k", dk_scales, range(0, 2))
-        nc.sync.dma_start(out=wq_w[0][:].bitcast(I32), in_=wq_words[0, 0].rearrange("p c d -> p (c d)").bitcast(I32))
-        load_table_scales("k", dk_scales, range(2, 4))
         load_table_words("k", dk_words)
-        nc.sync.dma_start(out=wv_first[0][:].bitcast(I32), in_=wv_words[0, 0, :, 0 * P : 2 * P].bitcast(I32))
+        load_table_scales("k", dk_scales, range(0, 4))
+        load_wk(0)
+        load_table_scales("v", dv_scales, range(0, 2))
+        nc.sync.dma_start(out=wv_all[0][:].bitcast(I32), in_=wv_words[0, 0].bitcast(I32))
+        load_table_scales("v", dv_scales, range(2, 4))
+        load_table_words("v", dv_words)
+        nc.sync.dma_start(out=wq_first[0][:].bitcast(I32), in_=wq_words[0, 0, :, 0 * P : 1 * P, :].rearrange("p c d -> p (c d)").bitcast(I32))
         load_weight_scales(nc.sync, wv_s, wv_scales, FIRST_ROW["wv"], range(0, 4))
         nc.sync.dma_start(out=gates[:, 0:C], in_=gate[:, 0:C])
         load_wk(1)
-        nc.sync.dma_start(out=wv_first[1][:].bitcast(I32), in_=wv_words[0, 0, :, 2 * P : 4 * P].bitcast(I32))
-        nc.sync.dma_start(out=wq_w[1][:].bitcast(I32), in_=wq_words[1, 0].rearrange("p c d -> p (c d)").bitcast(I32))
-        nc.sync.dma_start(out=wv_second[:].bitcast(I32), in_=wv_words[1, 0].bitcast(I32))
+        nc.sync.dma_start(out=wq_first[1][:].bitcast(I32), in_=wq_words[0, 0, :, 1 * P : 2 * P, :].rearrange("p c d -> p (c d)").bitcast(I32))
+        nc.sync.dma_start(out=wq_second[:].bitcast(I32), in_=wq_words[1, 0].rearrange("p c d -> p (c d)").bitcast(I32))
+        nc.sync.dma_start(out=wv_all[1][:].bitcast(I32), in_=wv_words[1, 0].bitcast(I32))
         nc.sync.dma_start(out=gates[:, C : 2 * C], in_=gate[:, C : 2 * C])
 
         def gather(table, dtype, name, lo, hi):
@@ -108,34 +109,45 @@ def tile_moe_qkb_kernel(tc, dq_words, dq_scales, dk_words, dk_scales, dv_words, 
 
         q_s = gather(table_s["q"], U8, "q_s", 0, E)
         q_w = gather(table_w["q"], U32, "q_w", 0, E)
-        v_w = gather(table_w["v"], U32, "v_w", 0, E)
-        v_s = gather(table_s["v"], U8, "v_s", 0, E)
-        k_s = [gather(table_s["k"], U8, "k_s0", 0, 1)]
+        k_w = gather(table_w["k"], U32, "k_w", 0, E)
+        k_s = gather(table_s["k"], U8, "k_s", 0, E)
+        v_s = [gather(table_s["v"], U8, "v_s0", 0, 1)]
         quantize_wk(0)
-        k_w = [gather(table_w["k"], U32, "k_w%d" % e, e, e + 1) for e in range(E)]
+        v_w = [gather(table_w["v"], U32, "v_w%d" % e, e, e + 1) for e in range(E)]
 
-        def products(e, b, bank):
+        def products(e, b):
             slots = slice(e * C, (e + 1) * C)
             cols = slice(b * P, (b + 1) * P)
-            sums = psum.tile([P, C], F32, name="sums%d" % bank)
-            nc.tensor.matmul_mx(out=sums[:], lhsT=wq_w[e][:, cols].bitcast(FP8X4), lhsT_scale=wq_s[FIRST_ROW["wq"] :, e, cols],
+            sums = psum.tile([P, C], F32, name="sums%d" % b)
+
+            def values(stop):
+                for h in range(C // P):
+                    half = slice(h * P, (h + 1) * P)
+                    nc.tensor.matmul_mx(out=sums[:, half], lhsT=wv_w[e, b].bitcast(FP4X4), lhsT_scale=wv_s[:, e, cols],
+                                        rhs=v_w[e][:, half].bitcast(FP8X4), rhs_scale=v_s[e][:, half],
+                                        start=False, stop=stop and h == C // P - 1)
+
+            def keys(stop):
+                nc.tensor.matmul_mx(out=sums[:], lhsT=wk_w[e][:, cols].bitcast(FP8X4), lhsT_scale=wk_s[e][:, cols],
+                                    rhs=k_w[:, slots].bitcast(FP8X4), rhs_scale=k_s[FIRST_ROW["k"] :, slots], start=False, stop=stop)
+
+            nc.tensor.matmul_mx(out=sums[:], lhsT=wq_w[e, b].bitcast(FP8X4), lhsT_scale=wq_s[FIRST_ROW["wq"] :, e, cols],
                                 rhs=q_w[:, slots].bitcast(FP8X4), rhs_scale=q_s[FIRST_ROW["q"] :, slots], start=True, stop=False)
-            for h in range(C // P):
-                half = slice(e * C + h * P, e * C + (h + 1) * P)
-                nc.tensor.matmul_mx(out=sums[:, h * P : (h + 1) * P], lhsT=wv_w[e, b].bitcast(FP4X4),
-                                    lhsT_scale=wv_s[:, e, cols], rhs=v_w[:, half].bitcast(FP8X4), rhs_scale=v_s[:, half],
-                                    start=False, stop=False)
+            if e == 0:
+                keys(False)
+                values(True)
+            else:
+                values(False)
+                keys(True)
             if (e, b) == (0, 0):
-                k_s.append(gather(table_s["k"], U8, "wv_first0", 1, 2))
-            nc.tensor.matmul_mx(out=sums[:], lhsT=wk_w[e][:, cols].bitcast(FP8X4), lhsT_scale=wk_s[e][:, cols],
-                                rhs=k_w[e][:].bitcast(FP8X4), rhs_scale=k_s[e][FIRST_ROW["k"] :, :], start=False, stop=True)
+                v_s.append(gather(table_s["v"], U8, "wq_first0", 1, 2))
             dx = tile([P, C], F32, "wk_raw1" if (e, b) == (0, 1) else "dx%d_%d" % (e, b))
             nc.scalar.copy(out=dx[:], in_=sums[:])
             nc.vector.tensor_tensor(result[b][:].indirect(offsets[:, e * LIST_COLS : (e + 1) * LIST_COLS]), dx[:], gates[:, slots], MULT)
 
         for e in range(E):
             for b in range(BANDS):
-                products(e, b, b)
+                products(e, b)
                 if (e, b) == (0, 0):
                     quantize_wk(1)
         for b in range(BANDS):

@@ -115,17 +115,18 @@ def tile_moe_qkb_kernel(tc, dq_words, dq_scales, dk_words, dk_scales, dv_words, 
         quantize_wk(0)
         v_w = [gather(table_w["v"], U32, "v_w%d" % e, e, e + 1) for e in range(E)]
 
-        def products(e, b):
-            slots = slice(e * C, (e + 1) * C)
+        def products(e, b, lo, hi, bank, dx):
+            own = slice(lo, hi)
+            slots = slice(e * C + lo, e * C + hi)
             cols = slice(b * P, (b + 1) * P)
-            sums = psum.tile([P, C], F32, name="sums%d" % b)
+            sums = psum.tile([P, hi - lo], F32, name="sums%d" % bank)
 
             def values(stop):
-                for h in range(C // P):
-                    half = slice(h * P, (h + 1) * P)
-                    nc.tensor.matmul_mx(out=sums[:, half], lhsT=wv_w[e, b].bitcast(FP4X4), lhsT_scale=wv_s[:, e, cols],
+                for h in range(lo, hi, P):
+                    half = slice(h, h + P)
+                    nc.tensor.matmul_mx(out=sums[:, h - lo : h - lo + P], lhsT=wv_w[e, b].bitcast(FP4X4), lhsT_scale=wv_s[:, e, cols],
                                         rhs=v_w[e][:, half].bitcast(FP8X4), rhs_scale=v_s[e][:, half],
-                                        start=False, stop=stop and h == C // P - 1)
+                                        start=False, stop=stop and h + P == hi)
 
             def keys(stop):
                 nc.tensor.matmul_mx(out=sums[:], lhsT=wk_w[e][:, cols].bitcast(FP8X4), lhsT_scale=wk_s[e][:, cols],
@@ -139,16 +140,23 @@ def tile_moe_qkb_kernel(tc, dq_words, dq_scales, dk_words, dk_scales, dv_words, 
             else:
                 values(False)
                 keys(True)
-            if (e, b) == (0, 0):
-                v_s.append(gather(table_s["v"], U8, "wq_first0", 1, 2))
-            dx = tile([P, C], F32, "wk_raw1" if (e, b) == (0, 1) else "dx%d_%d" % (e, b))
-            nc.scalar.copy(out=dx[:], in_=sums[:])
-            nc.vector.tensor_tensor(result[b][:].indirect(offsets[:, e * LIST_COLS : (e + 1) * LIST_COLS]), dx[:], gates[:, slots], MULT)
+            nc.scalar.copy(out=dx[:, own], in_=sums[:])
 
-        for e in range(E):
-            for b in range(BANDS):
-                products(e, b)
-                if (e, b) == (0, 0):
-                    quantize_wk(1)
+        def scatter(e, b, dx):
+            nc.vector.tensor_tensor(result[b][:].indirect(offsets[:, e * LIST_COLS : (e + 1) * LIST_COLS]), dx[:], gates[:, e * C : (e + 1) * C], MULT)
+
+        dx = tile([P, C], F32, "dx0_0")
+        products(0, 0, 0, P, 0, dx)
+        products(0, 0, P, C, 1, dx)
+        v_s.append(gather(table_s["v"], U8, "wq_first0", 1, 2))
+        scatter(0, 0, dx)
+        quantize_wk(1)
+        dx = tile([P, C], F32, "wk_raw1")
+        products(0, 1, 0, C, 0, dx)
+        scatter(0, 1, dx)
+        for b in range(BANDS):
+            dx = tile([P, C], F32, "dx1_%d" % b)
+            products(1, b, 0, C, 1 - b, dx)
+            scatter(1, b, dx)
         for b in range(BANDS):
             nc.sync.dma_start(out=out[b * P : (b + 1) * P, :], in_=result[b][:])

@@ -128,18 +128,26 @@ def tile_moe_qkb_kernel(tc, dq_words, dq_scales, dk_words, dk_scales, dv_words, 
                                         rhs=v_w[e][:, half].bitcast(FP8X4), rhs_scale=v_s[e][:, half],
                                         start=False, stop=stop and h + P == hi)
 
-            def keys(stop):
+            def keys(start, stop):
                 nc.tensor.matmul_mx(out=sums[:], lhsT=wk_w[e][:, cols].bitcast(FP8X4), lhsT_scale=wk_s[e][:, cols],
-                                    rhs=k_w[:, slots].bitcast(FP8X4), rhs_scale=k_s[FIRST_ROW["k"] :, slots], start=False, stop=stop)
+                                    rhs=k_w[:, slots].bitcast(FP8X4), rhs_scale=k_s[FIRST_ROW["k"] :, slots], start=start, stop=stop)
 
-            nc.tensor.matmul_mx(out=sums[:], lhsT=wq_w[e, b].bitcast(FP8X4), lhsT_scale=wq_s[FIRST_ROW["wq"] :, e, cols],
-                                rhs=q_w[:, slots].bitcast(FP8X4), rhs_scale=q_s[FIRST_ROW["q"] :, slots], start=True, stop=False)
-            if e == 0:
-                keys(False)
+            def queries(start, stop):
+                nc.tensor.matmul_mx(out=sums[:], lhsT=wq_w[e, b].bitcast(FP8X4), lhsT_scale=wq_s[FIRST_ROW["wq"] :, e, cols],
+                                    rhs=q_w[:, slots].bitcast(FP8X4), rhs_scale=q_s[FIRST_ROW["q"] :, slots], start=start, stop=stop)
+
+            if (e, b) == (0, 0):
+                keys(True, False)
+                queries(False, False)
                 values(True)
-            else:
+            elif e == 0:
+                keys(True, False)
                 values(False)
-                keys(True)
+                queries(False, True)
+            else:
+                queries(True, False)
+                values(False)
+                keys(False, True)
             nc.scalar.copy(out=dx[:, own], in_=sums[:])
 
         def scatter(e, b, dx):

@@ -14,6 +14,7 @@ U8 = mybir.dt.uint8
 FP8X4 = mybir.dt.float8_e4m3fn_x4
 FP4X4 = mybir.dt.float4_e2m1fn_x4
 MULT = mybir.AluOpType.mult
+COPY = mybir.ActivationFunctionType.Copy
 
 P = 128
 PACK = 4
@@ -27,6 +28,7 @@ def tile_moe_qkb_kernel(tc, dq_words, dq_scales, dk_words, dk_scales, dv_words, 
     nc = tc.nc
     with ExitStack() as ctx:
         keep = ctx.enter_context(tc.tile_pool(name="keep", bufs=1))
+        reused = ctx.enter_context(tc.tile_pool(name="reused", bufs=1))
         psum = ctx.enter_context(tc.psum_pool(name="psum", bufs=1))
 
         def tile(shape, dtype, name):
@@ -35,34 +37,29 @@ def tile_moe_qkb_kernel(tc, dq_words, dq_scales, dk_words, dk_scales, dv_words, 
         offsets = keep.tile([P, E * LIST_COLS], U16, name="offsets")
         table_w = {g: tile([P, T], U32, "table_w_" + g) for g in "qkv"}
         table_s = {g: tile([P, T], U8, "table_s_" + g) for g in "qkv"}
-        wq_first = [tile([P, P], U32, "wq_first%d" % b) for b in range(BANDS)]
-        wq_second = tile([P, K], U32, "wq_second")
-        wq_w = {(e, b): wq_second[:, b * P : (b + 1) * P] if e else wq_first[b][:] for e in range(E) for b in range(BANDS)}
+        wq_w = tile([P, E, K], U32, "wq_w")
         wq_s = tile([P, E, K], U8, "wq_s")
-        wv_all = [tile([P, 2 * K], U8, "wv_w%d" % e) for e in range(E)]
-        wv_w = {(e, b): wv_all[e][:, 2 * b * P : 2 * (b + 1) * P] for e in range(E) for b in range(BANDS)}
+        wv_w = tile([P, E, 2 * K], U8, "wv_w")
         wv_s = tile([P, E, K], U8, "wv_s")
         wk_raw = [tile([P, PACK, K], F32, "wk_raw%d" % e) for e in range(E)]
-        wk_bf = [tile([P, K * PACK], BF16, "wk_bf%d" % e) for e in range(E)]
+        wk_bf = [reused.tile([P, K * PACK], BF16, name="wk_bf0", align_bytes=64, offset=0), tile([P, K * PACK], BF16, "wk_bf1")]
         wk_w = [tile([P, K], U32, "wk_w%d" % e) for e in range(E)]
         wk_s = [tile([P, K], U8, "wk_s%d" % e) for e in range(E)]
         gates = tile([P, E * C], F32, "gates")
         result = [tile([P, T], F32, "result%d" % b) for b in range(BANDS)]
 
-        for g in "kv":
-            nc.vector.memset(table_s[g][:].bitcast(I32), 0)
+        nc.vector.memset(table_s["k"][:].bitcast(I32), 0)
+        nc.gpsimd.memset(table_s["v"][:].bitcast(I32), 0)
         zero = tile([P, 8], F32, "zero")
         nc.vector.memset(zero[:], 0.0)
-        for b in range(BANDS):
-            nc.scalar.copy(out=result[b][:], in_=zero[:, 0:1].to_broadcast([P, T]))
 
         def load_table_words(g, words):
             nc.sync.dma_start(out=table_w[g][:].bitcast(I32), in_=words[0].rearrange("p t d -> p (t d)").bitcast(I32))
 
-        def load_table_scales(g, scales, which):
+        def load_table_scales(queue, g, scales):
             rows = scales[0].rearrange("(q r) t -> r q t", r=4)
-            for r in which:
-                nc.sync.dma_start(out=table_s[g][FIRST_ROW[g] + r : P : QUAD, :].bitcast(I32), in_=rows[r].bitcast(I32))
+            for r in range(4):
+                queue.dma_start(out=table_s[g][FIRST_ROW[g] + r : P : QUAD, :].bitcast(I32), in_=rows[r].bitcast(I32))
 
         def load_weight_scales(queue, plane, scales, first, which=range(4)):
             rows = scales.rearrange("e s (q r) c -> r q (e s) c", r=4)
@@ -72,99 +69,81 @@ def tile_moe_qkb_kernel(tc, dq_words, dq_scales, dk_words, dk_scales, dv_words, 
         def load_wk(e):
             nc.sync.dma_start(out=wk_raw[e][:], in_=wk[e].rearrange("(p j) c -> p j c", j=PACK))
 
+        def load_wq():
+            nc.sync.dma_start(out=wq_w[:].bitcast(I32), in_=wq_words.rearrange("e s p c d -> p (e s) (c d)").bitcast(I32))
+
         for q in range(P // QUAD):
             rows = dq_scales[0, 4 * q : 4 * q + 4, :].bitcast(I32)
             queue = nc.sync if q < 2 else nc.scalar
             queue.dma_start(out=table_s["q"][q * QUAD : (q + 1) * QUAD, :].bitcast(I32), in_=rows.unsqueeze(0).to_broadcast([QUAD // 4, 4, T // 4]))
         nc.sync.dma_start(offsets[:], offs)
-        load_weight_scales(nc.gpsimd, wq_s, wq_scales, FIRST_ROW["wq"])
+        load_table_scales(nc.gpsimd, "v", dv_scales)
         load_table_words("q", dq_words)
         load_table_words("k", dk_words)
-        load_table_scales("k", dk_scales, range(0, 4))
+        load_table_scales(nc.sync, "k", dk_scales)
         load_wk(0)
-        load_table_scales("v", dv_scales, range(0, 2))
-        nc.sync.dma_start(out=wv_all[0][:].bitcast(I32), in_=wv_words[0, 0].bitcast(I32))
-        load_table_scales("v", dv_scales, range(2, 4))
         load_table_words("v", dv_words)
-        nc.sync.dma_start(out=wq_first[0][:].bitcast(I32), in_=wq_words[0, 0, :, 0 * P : 1 * P, :].rearrange("p c d -> p (c d)").bitcast(I32))
-        load_weight_scales(nc.sync, wv_s, wv_scales, FIRST_ROW["wv"], range(0, 4))
-        nc.sync.dma_start(out=gates[:, 0:C], in_=gate[:, 0:C])
+        load_weight_scales(nc.sync, wq_s, wq_scales, FIRST_ROW["wq"])
+        load_wq()
         load_wk(1)
-        nc.sync.dma_start(out=wq_first[1][:].bitcast(I32), in_=wq_words[0, 0, :, 1 * P : 2 * P, :].rearrange("p c d -> p (c d)").bitcast(I32))
-        nc.sync.dma_start(out=wq_second[:].bitcast(I32), in_=wq_words[1, 0].rearrange("p c d -> p (c d)").bitcast(I32))
-        nc.sync.dma_start(out=wv_all[1][:].bitcast(I32), in_=wv_words[1, 0].bitcast(I32))
-        nc.sync.dma_start(out=gates[:, C : 2 * C], in_=gate[:, C : 2 * C])
+        load_weight_scales(nc.sync, wv_s, wv_scales, FIRST_ROW["wv"])
+        nc.sync.dma_start(out=wv_w[:].bitcast(I32), in_=wv_words.rearrange("e s p c -> p (e s) c").bitcast(I32))
+        nc.sync.dma_start(out=gates[:], in_=gate)
 
-        def gather(table, dtype, name, lo, hi):
-            slots = tile([P, (hi - lo) * C], dtype, name)
-            nc.vector.tensor_copy(slots[:], table[:].indirect(offsets[:, lo * LIST_COLS : hi * LIST_COLS]))
+        for b in range(BANDS):
+            nc.scalar.activation(result[b][:], zero[:, 0:1].to_broadcast([P, T]), COPY)
+
+        def entries(lo, hi):
+            return offsets[:, lo * LIST_COLS : hi * LIST_COLS]
+
+        def gather(table, slots, lo, hi):
+            nc.vector.tensor_copy(slots[:], table[:].indirect(entries(lo, hi)))
             return slots
 
-        def quantize_wk(e):
-            nc.scalar.copy(
+        def round_wk(e):
+            nc.scalar.activation(
                 out=wk_bf[e][:].rearrange("p (c i j) -> p c j i", i=4, j=PACK),
                 in_=wk_raw[e][:].rearrange("p j (c i) -> p c j i", i=4),
+                func=COPY,
             )
+
+        def quantize_wk(e):
             nc.vector.quantize_mx(out=wk_w[e][:].bitcast(FP8X4), scales=wk_s[e][:], in_=wk_bf[e][:])
 
-        q_s = gather(table_s["q"], U8, "q_s", 0, E)
-        q_w = gather(table_w["q"], U32, "q_w", 0, E)
-        k_w = gather(table_w["k"], U32, "k_w", 0, E)
-        k_s = gather(table_s["k"], U8, "k_s", 0, E)
-        v_s = [gather(table_s["v"], U8, "v_s0", 0, 1)]
+        q_s = gather(table_s["q"], tile([P, E * C], U8, "q_s"), 0, E)
+        q_w = gather(table_w["q"], tile([P, E * C], U32, "q_w"), 0, E)
+        k_w = gather(table_w["k"], tile([P, E * C], U32, "k_w"), 0, E)
+        k_s = gather(table_s["k"], tile([P, E * C], U8, "k_s"), 0, E)
+        round_wk(0)
         quantize_wk(0)
-        v_w = [gather(table_w["v"], U32, "v_w%d" % e, e, e + 1) for e in range(E)]
-
-        def products(e, b, lo, hi, bank, dx):
-            own = slice(lo, hi)
-            slots = slice(e * C + lo, e * C + hi)
-            cols = slice(b * P, (b + 1) * P)
-            sums = psum.tile([P, hi - lo], F32, name="sums%d" % bank)
-
-            def values(stop):
-                for h in range(lo, hi, P):
-                    half = slice(h, h + P)
-                    nc.tensor.matmul_mx(out=sums[:, h - lo : h - lo + P], lhsT=wv_w[e, b].bitcast(FP4X4), lhsT_scale=wv_s[:, e, cols],
-                                        rhs=v_w[e][:, half].bitcast(FP8X4), rhs_scale=v_s[e][:, half],
-                                        start=False, stop=stop and h + P == hi)
-
-            def keys(start, stop):
-                nc.tensor.matmul_mx(out=sums[:], lhsT=wk_w[e][:, cols].bitcast(FP8X4), lhsT_scale=wk_s[e][:, cols],
-                                    rhs=k_w[:, slots].bitcast(FP8X4), rhs_scale=k_s[FIRST_ROW["k"] :, slots], start=start, stop=stop)
-
-            def queries(start, stop):
-                nc.tensor.matmul_mx(out=sums[:], lhsT=wq_w[e, b].bitcast(FP8X4), lhsT_scale=wq_s[FIRST_ROW["wq"] :, e, cols],
-                                    rhs=q_w[:, slots].bitcast(FP8X4), rhs_scale=q_s[FIRST_ROW["q"] :, slots], start=start, stop=stop)
-
-            if (e, b) == (0, 0):
-                keys(True, False)
-                queries(False, False)
-                values(True)
-            elif e == 0:
-                keys(True, False)
-                values(False)
-                queries(False, True)
-            else:
-                queries(True, False)
-                values(False)
-                keys(False, True)
-            nc.scalar.copy(out=dx[:, own], in_=sums[:])
-
-        def scatter(e, b, dx):
-            nc.vector.tensor_tensor(result[b][:].indirect(offsets[:, e * LIST_COLS : (e + 1) * LIST_COLS]), dx[:], gates[:, e * C : (e + 1) * C], MULT)
-
-        dx = tile([P, C], F32, "dx0_0")
-        products(0, 0, 0, P, 0, dx)
-        products(0, 0, P, C, 1, dx)
-        v_s.append(gather(table_s["v"], U8, "wq_first0", 1, 2))
-        scatter(0, 0, dx)
+        v_w = gather(table_w["v"], tile([P, E * C], U32, "wk_raw0"), 0, E)
+        v_s = [gather(table_s["v"], reused.tile([P, C], U8, name="v_s%d" % e, align_bytes=64, offset=e * C), e, e + 1) for e in range(E)]
+        round_wk(1)
         quantize_wk(1)
-        dx = tile([P, C], F32, "wk_raw1")
-        products(0, 1, 0, C, 0, dx)
-        scatter(0, 1, dx)
-        for b in range(BANDS):
-            dx = tile([P, C], F32, "dx1_%d" % b)
-            products(1, b, 0, C, 1 - b, dx)
-            scatter(1, b, dx)
+
+        def products(e, b, order):
+            slots = slice(e * C, (e + 1) * C)
+            cols = slice(b * P, (b + 1) * P)
+            sums = psum.tile([P, C], F32, name="sums%d_%d" % (e, b))
+            operands = {
+                "q": (wq_w[:, e, cols].bitcast(FP8X4), wq_s[FIRST_ROW["wq"] :, e, cols], q_w[:, slots], q_s[FIRST_ROW["q"] :, slots]),
+                "k": (wk_w[e][:, cols].bitcast(FP8X4), wk_s[e][:, cols], k_w[:, slots], k_s[FIRST_ROW["k"] :, slots]),
+                "v": (wv_w[:, e, 2 * b * P : 2 * (b + 1) * P].bitcast(FP4X4), wv_s[:, e, cols], v_w[:, slots], v_s[e][:]),
+            }
+            for g in order:
+                weights, weight_scales, words, scales = operands[g]
+                nc.tensor.matmul_mx(out=sums[:], lhsT=weights, lhsT_scale=weight_scales, rhs=words.bitcast(FP8X4), rhs_scale=scales,
+                                    start=g == order[0], stop=g == order[-1])
+            return sums
+
+        dx_low = [tile([P, C], F32, "dx_low%d" % e) for e in range(E)]
+        dx_high = tile([P, E * C], F32, "dx_high")
+        sums = [[products(e, b, "qvk" if e else "kqv") for b in range(BANDS)] for e in range(E)]
+        nc.scalar.copy(dx_high[:, 0:C], sums[0][1][:])
+        for e in range(E):
+            nc.vector.tensor_tensor(dx_low[e][:], sums[e][0][:], gates[:, e * C : (e + 1) * C], MULT)
+            nc.scalar.activation(result[0][:].indirect(entries(e, e + 1)), dx_low[e][:], COPY)
+        nc.vector.tensor_copy(dx_high[:, C : 2 * C], sums[1][1][:])
+        nc.vector.tensor_tensor(result[1][:].indirect(entries(0, E)), dx_high[:], gates[:], MULT)
         for b in range(BANDS):
             nc.sync.dma_start(out=out[b * P : (b + 1) * P, :], in_=result[b][:])

@@ -44,7 +44,7 @@ def tile_moe_qkb_kernel(tc, dq_words, dq_scales, dk_words, dk_scales, dv_words, 
         wk_raw = [tile([P, PACK, K], F32, "wk_raw%d" % e) for e in range(E)]
         wk_bf = [reused.tile([P, K * PACK], BF16, name="wk_bf0", align_bytes=64, offset=0), tile([P, K * PACK], BF16, "wk_bf1")]
         wk_w = [tile([P, K], U32, "wk_w%d" % e) for e in range(E)]
-        wk_s = [tile([P, K], U8, "wk_s%d" % e) for e in range(E)]
+        wk_s = [tile([P, K], U8, "wk_s0")]
         gates = tile([P, E * C], F32, "gates")
         result = [tile([P, T], F32, "result%d" % b) for b in range(BANDS)]
 
@@ -56,9 +56,9 @@ def tile_moe_qkb_kernel(tc, dq_words, dq_scales, dk_words, dk_scales, dv_words, 
         def load_table_words(g, words):
             nc.sync.dma_start(out=table_w[g][:].bitcast(I32), in_=words[0].rearrange("p t d -> p (t d)").bitcast(I32))
 
-        def load_table_scales(queue, g, scales):
+        def load_table_scales(queue, g, scales, which=range(4)):
             rows = scales[0].rearrange("(q r) t -> r q t", r=4)
-            for r in range(4):
+            for r in which:
                 queue.dma_start(out=table_s[g][FIRST_ROW[g] + r : P : QUAD, :].bitcast(I32), in_=rows[r].bitcast(I32))
 
         def load_weight_scales(queue, plane, scales, first, which=range(4)):
@@ -78,26 +78,31 @@ def tile_moe_qkb_kernel(tc, dq_words, dq_scales, dk_words, dk_scales, dv_words, 
             queue.dma_start(out=table_s["q"][q * QUAD : (q + 1) * QUAD, :].bitcast(I32), in_=rows.unsqueeze(0).to_broadcast([QUAD // 4, 4, T // 4]))
         nc.sync.dma_start(offsets[:], offs)
         load_table_scales(nc.gpsimd, "v", dv_scales)
+        load_table_scales(nc.sync, "k", dk_scales, range(0, 1))
         load_table_words("q", dq_words)
         load_table_words("k", dk_words)
-        load_table_scales(nc.sync, "k", dk_scales)
+        load_table_scales(nc.sync, "k", dk_scales, range(1, 4))
+        load_weight_scales(nc.sync, wq_s, wq_scales, FIRST_ROW["wq"], range(0, 2))
         load_wk(0)
         load_table_words("v", dv_words)
-        load_weight_scales(nc.sync, wq_s, wq_scales, FIRST_ROW["wq"])
+        load_weight_scales(nc.sync, wq_s, wq_scales, FIRST_ROW["wq"], range(2, 4))
+        load_weight_scales(nc.sync, wv_s, wv_scales, FIRST_ROW["wv"], range(0, 2))
         load_wq()
-        load_wk(1)
-        load_weight_scales(nc.sync, wv_s, wv_scales, FIRST_ROW["wv"])
         nc.sync.dma_start(out=wv_w[:].bitcast(I32), in_=wv_words.rearrange("e s p c -> p (e s) c").bitcast(I32))
-        nc.sync.dma_start(out=gates[:], in_=gate)
+        load_wk(1)
+        load_weight_scales(nc.sync, wv_s, wv_scales, FIRST_ROW["wv"], range(2, 3))
+        nc.sync.dma_start(out=gates[:, 0:C], in_=gate[:, 0:C])
+        load_weight_scales(nc.sync, wv_s, wv_scales, FIRST_ROW["wv"], range(3, 4))
+        nc.sync.dma_start(out=gates[:, C : 2 * C], in_=gate[:, C : 2 * C])
 
         for b in range(BANDS):
             nc.scalar.activation(result[b][:], zero[:, 0:1].to_broadcast([P, T]), COPY)
 
         def entries(lo, hi):
-            return offsets[:, lo * LIST_COLS : hi * LIST_COLS]
+            return offsets[:, lo // 16 : hi // 16]
 
         def gather(table, slots, lo, hi):
-            nc.vector.tensor_copy(slots[:], table[:].indirect(entries(lo, hi)))
+            nc.vector.tensor_copy(slots[:], table[:].indirect(entries(lo * C, hi * C)))
             return slots
 
         def round_wk(e):
@@ -114,12 +119,13 @@ def tile_moe_qkb_kernel(tc, dq_words, dq_scales, dk_words, dk_scales, dv_words, 
         q_w = gather(table_w["q"], tile([P, E * C], U32, "q_w"), 0, E)
         k_w = gather(table_w["k"], tile([P, E * C], U32, "k_w"), 0, E)
         k_s = gather(table_s["k"], tile([P, E * C], U8, "k_s"), 0, E)
+        v_w = [gather(table_w["v"], tile([P, C], U32, "v_w0"), 0, 1)]
         round_wk(0)
         quantize_wk(0)
-        v_w = gather(table_w["v"], tile([P, E * C], U32, "wk_raw0"), 0, E)
-        v_s = [gather(table_s["v"], reused.tile([P, C], U8, name="v_s%d" % e, align_bytes=64, offset=e * C), e, e + 1) for e in range(E)]
+        v_s = [gather(table_s["v"], tile([P, C], U8, "wk_raw0"), 0, 1)]
+        v_w.append(gather(table_w["v"], reused.tile([P, C], U32, name="v_w1", align_bytes=64, offset=E * C), 1, 2))
+        v_s.append(gather(table_s["v"], reused.tile([P, C], U8, name="v_s1", align_bytes=64, offset=C), 1, 2))
         round_wk(1)
-        quantize_wk(1)
 
         def products(e, b, order):
             slots = slice(e * C, (e + 1) * C)
@@ -128,7 +134,7 @@ def tile_moe_qkb_kernel(tc, dq_words, dq_scales, dk_words, dk_scales, dv_words, 
             operands = {
                 "q": (wq_w[:, e, cols].bitcast(FP8X4), wq_s[FIRST_ROW["wq"] :, e, cols], q_w[:, slots], q_s[FIRST_ROW["q"] :, slots]),
                 "k": (wk_w[e][:, cols].bitcast(FP8X4), wk_s[e][:, cols], k_w[:, slots], k_s[FIRST_ROW["k"] :, slots]),
-                "v": (wv_w[:, e, 2 * b * P : 2 * (b + 1) * P].bitcast(FP4X4), wv_s[:, e, cols], v_w[:, slots], v_s[e][:]),
+                "v": (wv_w[:, e, 2 * b * P : 2 * (b + 1) * P].bitcast(FP4X4), wv_s[:, e, cols], v_w[e][:], v_s[e][:]),
             }
             for g in order:
                 weights, weight_scales, words, scales = operands[g]
@@ -138,12 +144,23 @@ def tile_moe_qkb_kernel(tc, dq_words, dq_scales, dk_words, dk_scales, dv_words, 
 
         dx_low = [tile([P, C], F32, "dx_low%d" % e) for e in range(E)]
         dx_high = tile([P, E * C], F32, "dx_high")
-        sums = [[products(e, b, "qvk" if e else "kqv") for b in range(BANDS)] for e in range(E)]
-        nc.scalar.copy(dx_high[:, 0:C], sums[0][1][:])
-        for e in range(E):
-            nc.vector.tensor_tensor(dx_low[e][:], sums[e][0][:], gates[:, e * C : (e + 1) * C], MULT)
-            nc.scalar.activation(result[0][:].indirect(entries(e, e + 1)), dx_low[e][:], COPY)
-        nc.vector.tensor_copy(dx_high[:, C : 2 * C], sums[1][1][:])
-        nc.vector.tensor_tensor(result[1][:].indirect(entries(0, E)), dx_high[:], gates[:], MULT)
+
+        def low_band(e, sums):
+            nc.vector.tensor_tensor(dx_low[e][:], sums[:], gates[:, e * C : (e + 1) * C], MULT)
+            nc.scalar.activation(result[0][:].indirect(entries(e * C, (e + 1) * C)), dx_low[e][:], COPY)
+
+        def high_band(lo, hi):
+            nc.vector.tensor_tensor(result[1][:].indirect(entries(lo, hi)), dx_high[:, lo:hi], gates[:, lo:hi], MULT)
+
+        first = [products(0, b, "kqv") for b in range(BANDS)]
+        nc.scalar.copy(dx_high[:, 0:C], first[1][:])
+        low_band(0, first[0])
+        wk_s.append(tile([P, K], U8, "v_w0"))
+        quantize_wk(1)
+        high_band(0, P)
+        second = [products(1, b, "qvk") for b in range(BANDS)]
+        low_band(1, second[0])
+        nc.vector.tensor_copy(dx_high[:, C : 2 * C], second[1][:])
+        high_band(P, E * C)
         for b in range(BANDS):
             nc.sync.dma_start(out=out[b * P : (b + 1) * P, :], in_=result[b][:])

@@ -20,29 +20,28 @@ P = 128
 PACK = 4
 QUAD = 32
 BANDS = K // P
-LIST_COLS = C // 16
-FIRST_ROW = {"q": 4, "k": 12, "v": 0, "wq": 8, "wv": 0}
+FIRST_ROW = {"k": 12, "v": 0}
+WQ_FIRST_ROW = (0, 12)
 
 
 def tile_moe_qkb_kernel(tc, dq_words, dq_scales, dk_words, dk_scales, dv_words, dv_scales, wq_words, wq_scales, wk, wv_words, wv_scales, gate, offs, out):
     nc = tc.nc
     with ExitStack() as ctx:
         keep = ctx.enter_context(tc.tile_pool(name="keep", bufs=1))
-        reused = ctx.enter_context(tc.tile_pool(name="reused", bufs=1))
         psum = ctx.enter_context(tc.psum_pool(name="psum", bufs=1))
 
         def tile(shape, dtype, name):
             return keep.tile(shape, dtype, name=name, align_bytes=64)
 
-        offsets = keep.tile([P, E * LIST_COLS], U16, name="offsets")
+        offsets = keep.tile([P, E * C // 16], U16, name="offsets")
         table_w = {g: tile([P, T], U32, "table_w_" + g) for g in "qkv"}
         table_s = {g: tile([P, T], U8, "table_s_" + g) for g in "qkv"}
-        wq_w = tile([P, E, K], U32, "wq_w")
-        wq_s = tile([P, E, K], U8, "wq_s")
-        wv_w = tile([P, E, 2 * K], U8, "wv_w")
-        wv_s = tile([P, E, K], U8, "wv_s")
+        wq_w = [tile([P, K], U32, "wq_w%d" % e) for e in range(E)]
+        wq_s = [tile([P, K], U8, "wq_s%d" % e) for e in range(E)]
+        wv_w = [tile([P, 2 * K], U8, "wv_w%d" % e) for e in range(E)]
+        wv_s = [tile([P, K], U8, "wv_s%d" % e) for e in range(E)]
         wk_raw = [tile([P, PACK, K], F32, "wk_raw%d" % e) for e in range(E)]
-        wk_bf = [reused.tile([P, K * PACK], BF16, name="wk_bf0", align_bytes=64, offset=0), tile([P, K * PACK], BF16, "wk_bf1")]
+        wk_bf = [tile([P, K * PACK], BF16, "wk_bf%d" % e) for e in range(E)]
         wk_w = [tile([P, K], U32, "wk_w%d" % e) for e in range(E)]
         wk_s = [tile([P, K], U8, "wk_s0")]
         gates = tile([P, E * C], F32, "gates")
@@ -56,21 +55,26 @@ def tile_moe_qkb_kernel(tc, dq_words, dq_scales, dk_words, dk_scales, dv_words, 
         def load_table_words(g, words):
             nc.sync.dma_start(out=table_w[g][:].bitcast(I32), in_=words[0].rearrange("p t d -> p (t d)").bitcast(I32))
 
-        def load_table_scales(queue, g, scales, which=range(4)):
+        def load_table_scales(queue, g, scales):
             rows = scales[0].rearrange("(q r) t -> r q t", r=4)
-            for r in which:
+            for r in range(4):
                 queue.dma_start(out=table_s[g][FIRST_ROW[g] + r : P : QUAD, :].bitcast(I32), in_=rows[r].bitcast(I32))
 
-        def load_weight_scales(queue, plane, scales, first, which=range(4)):
-            rows = scales.rearrange("e s (q r) c -> r q (e s) c", r=4)
-            for r in which:
-                queue.dma_start(out=plane[first + r : P : QUAD, :, :].bitcast(I32), in_=rows[r].bitcast(I32))
+        def load_periodic(plane, scales, first, period, repeats):
+            rows = scales.rearrange("e s b c -> (e s b) c").bitcast(I32)[first : first + period, :]
+            nc.sync.dma_start(out=plane[0 : repeats * period, :].bitcast(I32), in_=rows.unsqueeze(0).to_broadcast([repeats, period, K // 4]))
 
         def load_wk(e):
             nc.sync.dma_start(out=wk_raw[e][:], in_=wk[e].rearrange("(p j) c -> p j c", j=PACK))
 
-        def load_wq():
-            nc.sync.dma_start(out=wq_w[:].bitcast(I32), in_=wq_words.rearrange("e s p c d -> p (e s) (c d)").bitcast(I32))
+        def load_wq(e):
+            nc.sync.dma_start(out=wq_w[e][:].bitcast(I32), in_=wq_words[e, 0].rearrange("p c d -> p (c d)").bitcast(I32))
+
+        def load_wv(e):
+            nc.sync.dma_start(out=wv_w[e][:].bitcast(I32), in_=wv_words[e, 0].bitcast(I32))
+
+        def load_gate(e):
+            nc.sync.dma_start(out=gates[:, e * C : (e + 1) * C], in_=gate[:, e * C : (e + 1) * C])
 
         for q in range(P // QUAD):
             rows = dq_scales[0, 4 * q : 4 * q + 4, :].bitcast(I32)
@@ -78,22 +82,23 @@ def tile_moe_qkb_kernel(tc, dq_words, dq_scales, dk_words, dk_scales, dv_words, 
             queue.dma_start(out=table_s["q"][q * QUAD : (q + 1) * QUAD, :].bitcast(I32), in_=rows.unsqueeze(0).to_broadcast([QUAD // 4, 4, T // 4]))
         nc.sync.dma_start(offsets[:], offs)
         load_table_scales(nc.gpsimd, "v", dv_scales)
-        load_table_scales(nc.sync, "k", dk_scales, range(0, 1))
         load_table_words("q", dq_words)
         load_table_words("k", dk_words)
-        load_table_scales(nc.sync, "k", dk_scales, range(1, 4))
-        load_weight_scales(nc.sync, wq_s, wq_scales, FIRST_ROW["wq"], range(0, 2))
+        load_table_scales(nc.sync, "k", dk_scales)
         load_wk(0)
+        load_periodic(wq_s[0], wq_scales, 0, 28, 4)
         load_table_words("v", dv_words)
-        load_weight_scales(nc.sync, wq_s, wq_scales, FIRST_ROW["wq"], range(2, 4))
-        load_weight_scales(nc.sync, wv_s, wv_scales, FIRST_ROW["wv"], range(0, 2))
-        load_wq()
-        nc.sync.dma_start(out=wv_w[:].bitcast(I32), in_=wv_words.rearrange("e s p c -> p (e s) c").bitcast(I32))
+        load_wq(0)
         load_wk(1)
-        load_weight_scales(nc.sync, wv_s, wv_scales, FIRST_ROW["wv"], range(2, 3))
-        nc.sync.dma_start(out=gates[:, 0:C], in_=gate[:, 0:C])
-        load_weight_scales(nc.sync, wv_s, wv_scales, FIRST_ROW["wv"], range(3, 4))
-        nc.sync.dma_start(out=gates[:, C : 2 * C], in_=gate[:, C : 2 * C])
+        load_periodic(wv_s[0], wv_scales, 0, 28, 4)
+        load_gate(0)
+        load_wv(0)
+        load_wq(1)
+        load_periodic(wv_s[1], wv_scales, 16, 14, 7)
+        load_periodic(wq_s[1], wq_scales, 4, 28, 4)
+        load_wv(1)
+        nc.sync.dma_start(out=wv_s[1][98:100, :].bitcast(I32), in_=wv_scales[1, 0, 14:16, :].bitcast(I32))
+        load_gate(1)
 
         for b in range(BANDS):
             nc.scalar.activation(result[b][:], zero[:, 0:1].to_broadcast([P, T]), COPY)
@@ -123,8 +128,6 @@ def tile_moe_qkb_kernel(tc, dq_words, dq_scales, dk_words, dk_scales, dv_words, 
         round_wk(0)
         quantize_wk(0)
         v_s = [gather(table_s["v"], tile([P, C], U8, "wk_raw0"), 0, 1)]
-        v_w.append(gather(table_w["v"], reused.tile([P, C], U32, name="v_w1", align_bytes=64, offset=E * C), 1, 2))
-        v_s.append(gather(table_s["v"], reused.tile([P, C], U8, name="v_s1", align_bytes=64, offset=C), 1, 2))
         round_wk(1)
 
         def products(e, b, order):
@@ -132,9 +135,9 @@ def tile_moe_qkb_kernel(tc, dq_words, dq_scales, dk_words, dk_scales, dv_words, 
             cols = slice(b * P, (b + 1) * P)
             sums = psum.tile([P, C], F32, name="sums%d_%d" % (e, b))
             operands = {
-                "q": (wq_w[:, e, cols].bitcast(FP8X4), wq_s[FIRST_ROW["wq"] :, e, cols], q_w[:, slots], q_s[FIRST_ROW["q"] :, slots]),
+                "q": (wq_w[e][:, cols].bitcast(FP8X4), wq_s[e][WQ_FIRST_ROW[e] :, cols], q_w[:, slots], q_s[:, slots]),
                 "k": (wk_w[e][:, cols].bitcast(FP8X4), wk_s[e][:, cols], k_w[:, slots], k_s[FIRST_ROW["k"] :, slots]),
-                "v": (wv_w[:, e, 2 * b * P : 2 * (b + 1) * P].bitcast(FP4X4), wv_s[:, e, cols], v_w[e][:], v_s[e][:]),
+                "v": (wv_w[e][:, 2 * b * P : 2 * (b + 1) * P].bitcast(FP4X4), wv_s[e][:, cols], v_w[e][:], v_s[e][:]),
             }
             for g in order:
                 weights, weight_scales, words, scales = operands[g]
@@ -152,9 +155,11 @@ def tile_moe_qkb_kernel(tc, dq_words, dq_scales, dk_words, dk_scales, dv_words, 
         def high_band(lo, hi):
             nc.vector.tensor_tensor(result[1][:].indirect(entries(lo, hi)), dx_high[:, lo:hi], gates[:, lo:hi], MULT)
 
-        first = [products(0, b, "kqv") for b in range(BANDS)]
+        first = [products(0, b, "qkv") for b in range(BANDS)]
+        v_w.append(gather(table_w["v"], tile([P, C], U32, "wk_bf0"), 1, 2))
         nc.scalar.copy(dx_high[:, 0:C], first[1][:])
         low_band(0, first[0])
+        v_s.append(gather(table_s["v"], tile([P, C], U8, "wv_w0"), 1, 2))
         wk_s.append(tile([P, K], U8, "v_w0"))
         quantize_wk(1)
         high_band(0, P)

@@ -55,9 +55,9 @@ def tile_moe_qkb_kernel(tc, dq_words, dq_scales, dk_words, dk_scales, dv_words, 
         def load_table_words(g, words):
             nc.sync.dma_start(out=table_w[g][:].bitcast(I32), in_=words[0].rearrange("p t d -> p (t d)").bitcast(I32))
 
-        def load_table_scales(queue, g, scales):
+        def load_table_scales(queue, g, scales, which=range(4)):
             rows = scales[0].rearrange("(q r) t -> r q t", r=4)
-            for r in range(4):
+            for r in which:
                 queue.dma_start(out=table_s[g][FIRST_ROW[g] + r : P : QUAD, :].bitcast(I32), in_=rows[r].bitcast(I32))
 
         def load_periodic(plane, scales, first, period, repeats):
@@ -81,13 +81,14 @@ def tile_moe_qkb_kernel(tc, dq_words, dq_scales, dk_words, dk_scales, dv_words, 
             queue = nc.sync if q < 2 else nc.scalar
             queue.dma_start(out=table_s["q"][q * QUAD : (q + 1) * QUAD, :].bitcast(I32), in_=rows.unsqueeze(0).to_broadcast([QUAD // 4, 4, T // 4]))
         nc.sync.dma_start(offsets[:], offs)
-        load_table_scales(nc.gpsimd, "v", dv_scales)
+        load_table_scales(nc.gpsimd, "v", dv_scales, range(0, 2))
         load_table_words("q", dq_words)
         load_table_words("k", dk_words)
         load_table_scales(nc.sync, "k", dk_scales)
         load_wk(0)
         load_periodic(wq_s[0], wq_scales, 0, 28, 4)
         load_table_words("v", dv_words)
+        load_table_scales(nc.sync, "v", dv_scales, range(2, 4))
         load_wq(0)
         load_wk(1)
         load_periodic(wv_s[0], wv_scales, 0, 28, 4)
@@ -156,7 +157,7 @@ def tile_moe_qkb_kernel(tc, dq_words, dq_scales, dk_words, dk_scales, dv_words, 
             nc.vector.tensor_tensor(result[1][:].indirect(entries(lo, hi)), dx_high[:, lo:hi], gates[:, lo:hi], MULT)
 
         first = [products(0, b, "qkv") for b in range(BANDS)]
-        v_w.append(gather(table_w["v"], tile([P, C], U32, "wk_bf0"), 1, 2))
+        v_w.append(gather(table_w["v"], tile([P, C], U32, "wq_w0"), 1, 2))
         nc.scalar.copy(dx_high[:, 0:C], first[1][:])
         low_band(0, first[0])
         v_s.append(gather(table_s["v"], tile([P, C], U8, "wv_w0"), 1, 2))

@@ -20,8 +20,7 @@ P = 128
 PACK = 4
 QUAD = 32
 BANDS = K // P
-FIRST_ROW = {"k": 12, "v": 0}
-WQ_FIRST_ROW = (0, 12)
+FIRST_ROW = {"q": 4, "k": 12, "v": 0, "wq": 8, "wv": 0}
 
 
 def tile_moe_qkb_kernel(tc, dq_words, dq_scales, dk_words, dk_scales, dv_words, dv_scales, wq_words, wq_scales, wk, wv_words, wv_scales, gate, offs, out):
@@ -37,9 +36,9 @@ def tile_moe_qkb_kernel(tc, dq_words, dq_scales, dk_words, dk_scales, dv_words, 
         table_w = {g: tile([P, T], U32, "table_w_" + g) for g in "qkv"}
         table_s = {g: tile([P, T], U8, "table_s_" + g) for g in "qkv"}
         wq_w = [tile([P, K], U32, "wq_w%d" % e) for e in range(E)]
-        wq_s = [tile([P, K], U8, "wq_s%d" % e) for e in range(E)]
+        wq_s = tile([P, E, K], U8, "wq_s")
         wv_w = [tile([P, 2 * K], U8, "wv_w%d" % e) for e in range(E)]
-        wv_s = [tile([P, K], U8, "wv_s%d" % e) for e in range(E)]
+        wv_s = tile([P, E, K], U8, "wv_s")
         wk_raw = [tile([P, PACK, K], F32, "wk_raw%d" % e) for e in range(E)]
         wk_bf = [tile([P, K * PACK], BF16, "wk_bf%d" % e) for e in range(E)]
         wk_w = [tile([P, K], U32, "wk_w%d" % e) for e in range(E)]
@@ -48,7 +47,7 @@ def tile_moe_qkb_kernel(tc, dq_words, dq_scales, dk_words, dk_scales, dv_words, 
         result = [tile([P, T], F32, "result%d" % b) for b in range(BANDS)]
 
         nc.vector.memset(table_s["k"][:].bitcast(I32), 0)
-        nc.gpsimd.memset(table_s["v"][:].bitcast(I32), 0)
+        nc.vector.memset(table_s["v"][:].bitcast(I32), 0)
         zero = tile([P, 8], F32, "zero")
         nc.vector.memset(zero[:], 0.0)
 
@@ -60,9 +59,10 @@ def tile_moe_qkb_kernel(tc, dq_words, dq_scales, dk_words, dk_scales, dv_words, 
             for r in which:
                 queue.dma_start(out=table_s[g][FIRST_ROW[g] + r : P : QUAD, :].bitcast(I32), in_=rows[r].bitcast(I32))
 
-        def load_periodic(plane, scales, first, period, repeats):
-            rows = scales.rearrange("e s b c -> (e s b) c").bitcast(I32)[first : first + period, :]
-            nc.sync.dma_start(out=plane[0 : repeats * period, :].bitcast(I32), in_=rows.unsqueeze(0).to_broadcast([repeats, period, K // 4]))
+        def load_weight_scales(queue, plane, scales, first):
+            rows = scales.rearrange("e s (q r) c -> r q (e s) c", r=4)
+            for r in range(4):
+                queue.dma_start(out=plane[first + r : P : QUAD, :, :].bitcast(I32), in_=rows[r].bitcast(I32))
 
         def load_wk(e):
             nc.sync.dma_start(out=wk_raw[e][:], in_=wk[e].rearrange("(p j) c -> p j c", j=PACK))
@@ -81,24 +81,21 @@ def tile_moe_qkb_kernel(tc, dq_words, dq_scales, dk_words, dk_scales, dv_words, 
             queue = nc.sync if q < 2 else nc.scalar
             queue.dma_start(out=table_s["q"][q * QUAD : (q + 1) * QUAD, :].bitcast(I32), in_=rows.unsqueeze(0).to_broadcast([QUAD // 4, 4, T // 4]))
         nc.sync.dma_start(offsets[:], offs)
-        load_table_scales(nc.gpsimd, "v", dv_scales, range(0, 2))
+        load_weight_scales(nc.gpsimd, wq_s, wq_scales, FIRST_ROW["wq"])
+        load_weight_scales(nc.gpsimd, wv_s, wv_scales, FIRST_ROW["wv"])
         load_table_words("q", dq_words)
         load_table_words("k", dk_words)
         load_table_scales(nc.sync, "k", dk_scales)
+        load_table_scales(nc.sync, "v", dv_scales, range(0, 1))
         load_wk(0)
-        load_periodic(wq_s[0], wq_scales, 0, 28, 4)
         load_table_words("v", dv_words)
-        load_table_scales(nc.sync, "v", dv_scales, range(2, 4))
+        load_table_scales(nc.sync, "v", dv_scales, range(1, 4))
         load_wq(0)
         load_wk(1)
-        load_periodic(wv_s[0], wv_scales, 0, 28, 4)
         load_gate(0)
         load_wv(0)
         load_wq(1)
-        load_periodic(wv_s[1], wv_scales, 16, 14, 7)
-        load_periodic(wq_s[1], wq_scales, 4, 28, 4)
         load_wv(1)
-        nc.sync.dma_start(out=wv_s[1][98:100, :].bitcast(I32), in_=wv_scales[1, 0, 14:16, :].bitcast(I32))
         load_gate(1)
 
         for b in range(BANDS):
@@ -131,19 +128,20 @@ def tile_moe_qkb_kernel(tc, dq_words, dq_scales, dk_words, dk_scales, dv_words, 
         v_s = [gather(table_s["v"], tile([P, C], U8, "wk_raw0"), 0, 1)]
         round_wk(1)
 
-        def products(e, b, order):
+        def products(e, order):
             slots = slice(e * C, (e + 1) * C)
-            cols = slice(b * P, (b + 1) * P)
-            sums = psum.tile([P, C], F32, name="sums%d_%d" % (e, b))
-            operands = {
-                "q": (wq_w[e][:, cols].bitcast(FP8X4), wq_s[e][WQ_FIRST_ROW[e] :, cols], q_w[:, slots], q_s[:, slots]),
-                "k": (wk_w[e][:, cols].bitcast(FP8X4), wk_s[e][:, cols], k_w[:, slots], k_s[FIRST_ROW["k"] :, slots]),
-                "v": (wv_w[e][:, 2 * b * P : 2 * (b + 1) * P].bitcast(FP4X4), wv_s[e][:, cols], v_w[e][:], v_s[e][:]),
-            }
+            sums = [psum.tile([P, C], F32, name="sums%d_%d" % (e, b)) for b in range(BANDS)]
             for g in order:
-                weights, weight_scales, words, scales = operands[g]
-                nc.tensor.matmul_mx(out=sums[:], lhsT=weights, lhsT_scale=weight_scales, rhs=words.bitcast(FP8X4), rhs_scale=scales,
-                                    start=g == order[0], stop=g == order[-1])
+                for b in range(BANDS):
+                    cols = slice(b * P, (b + 1) * P)
+                    if g == "q":
+                        weights, weight_scales, words, scales = wq_w[e][:, cols].bitcast(FP8X4), wq_s[FIRST_ROW["wq"] :, e, cols], q_w[:, slots], q_s[FIRST_ROW["q"] :, slots]
+                    elif g == "k":
+                        weights, weight_scales, words, scales = wk_w[e][:, cols].bitcast(FP8X4), wk_s[e][:, cols], k_w[:, slots], k_s[FIRST_ROW["k"] :, slots]
+                    else:
+                        weights, weight_scales, words, scales = wv_w[e][:, 2 * b * P : 2 * (b + 1) * P].bitcast(FP4X4), wv_s[:, e, cols], v_w[e][:], v_s[e][:]
+                    nc.tensor.matmul_mx(out=sums[b][:], lhsT=weights, lhsT_scale=weight_scales, rhs=words.bitcast(FP8X4), rhs_scale=scales,
+                                        start=g == order[0], stop=g == order[-1])
             return sums
 
         dx_low = [tile([P, C], F32, "dx_low%d" % e) for e in range(E)]
@@ -156,7 +154,7 @@ def tile_moe_qkb_kernel(tc, dq_words, dq_scales, dk_words, dk_scales, dv_words, 
         def high_band(lo, hi):
             nc.vector.tensor_tensor(result[1][:].indirect(entries(lo, hi)), dx_high[:, lo:hi], gates[:, lo:hi], MULT)
 
-        first = [products(0, b, "qkv") for b in range(BANDS)]
+        first = products(0, "qkv")
         v_w.append(gather(table_w["v"], tile([P, C], U32, "wq_w0"), 1, 2))
         nc.scalar.copy(dx_high[:, 0:C], first[1][:])
         low_band(0, first[0])
@@ -164,9 +162,9 @@ def tile_moe_qkb_kernel(tc, dq_words, dq_scales, dk_words, dk_scales, dv_words, 
         wk_s.append(tile([P, K], U8, "v_w0"))
         quantize_wk(1)
         high_band(0, P)
-        second = [products(1, b, "qvk") for b in range(BANDS)]
+        second = products(1, "qvk")
+        nc.scalar.copy(dx_high[:, C : 2 * C], second[1][:])
         low_band(1, second[0])
-        nc.vector.tensor_copy(dx_high[:, C : 2 * C], second[1][:])
         high_band(P, E * C)
         for b in range(BANDS):
             nc.sync.dma_start(out=out[b * P : (b + 1) * P, :], in_=result[b][:])

@@ -59,9 +59,9 @@ def tile_moe_qkb_kernel(tc, dq_words, dq_scales, dk_words, dk_scales, dv_words, 
             for r in which:
                 queue.dma_start(out=table_s[g][FIRST_ROW[g] + r : P : QUAD, :].bitcast(I32), in_=rows[r].bitcast(I32))
 
-        def load_weight_scales(queue, plane, scales, first):
+        def load_weight_scales(queue, plane, scales, first, which=range(4)):
             rows = scales.rearrange("e s (q r) c -> r q (e s) c", r=4)
-            for r in range(4):
+            for r in which:
                 queue.dma_start(out=plane[first + r : P : QUAD, :, :].bitcast(I32), in_=rows[r].bitcast(I32))
 
         def load_wk(e):
@@ -82,7 +82,7 @@ def tile_moe_qkb_kernel(tc, dq_words, dq_scales, dk_words, dk_scales, dv_words, 
             queue.dma_start(out=table_s["q"][q * QUAD : (q + 1) * QUAD, :].bitcast(I32), in_=rows.unsqueeze(0).to_broadcast([QUAD // 4, 4, T // 4]))
         nc.sync.dma_start(offsets[:], offs)
         load_weight_scales(nc.gpsimd, wq_s, wq_scales, FIRST_ROW["wq"])
-        load_weight_scales(nc.gpsimd, wv_s, wv_scales, FIRST_ROW["wv"])
+        load_weight_scales(nc.gpsimd, wv_s, wv_scales, FIRST_ROW["wv"], range(0, 2))
         load_table_words("q", dq_words)
         load_table_words("k", dk_words)
         load_table_scales(nc.sync, "k", dk_scales)
@@ -94,6 +94,7 @@ def tile_moe_qkb_kernel(tc, dq_words, dq_scales, dk_words, dk_scales, dv_words, 
         load_wk(1)
         load_gate(0)
         load_wv(0)
+        load_weight_scales(nc.sync, wv_s, wv_scales, FIRST_ROW["wv"], range(2, 4))
         load_wq(1)
         load_wv(1)
         load_gate(1)

@@ -48,7 +48,7 @@ def tile_moe_qkb_kernel(tc, dq_words, dq_scales, dk_words, dk_scales, dv_words, 
 
         nc.vector.memset(table_s["k"][:].bitcast(I32), 0)
         nc.vector.memset(table_s["v"][:].bitcast(I32), 0)
-        zero = tile([P, 8], F32, "zero")
+        zero = tile([P, 1], F32, "zero")
         nc.vector.memset(zero[:], 0.0)
 
         def load_table_words(g, words):
@@ -100,7 +100,7 @@ def tile_moe_qkb_kernel(tc, dq_words, dq_scales, dk_words, dk_scales, dv_words, 
         load_gate(1)
 
         for b in range(BANDS):
-            nc.scalar.activation(result[b][:], zero[:, 0:1].to_broadcast([P, T]), COPY)
+            nc.scalar.activation(result[b][:], zero[:].to_broadcast([P, T]), COPY)
 
         def entries(lo, hi):
             return offsets[:, lo // 16 : hi // 16]

@@ -106,7 +106,7 @@ def tile_moe_qkb_kernel(tc, dq_words, dq_scales, dk_words, dk_scales, dv_words, 
             return offsets[:, lo // 16 : hi // 16]
 
         def gather(table, slots, lo, hi):
-            nc.vector.tensor_copy(slots[:], table[:].indirect(entries(lo * C, hi * C)))
+            nc.vector.tensor_copy(slots[:], table[:].indirect(entries(lo, hi)))
             return slots
 
         def round_wk(e):
@@ -119,14 +119,14 @@ def tile_moe_qkb_kernel(tc, dq_words, dq_scales, dk_words, dk_scales, dv_words, 
         def quantize_wk(e):
             nc.vector.quantize_mx(out=wk_w[e][:].bitcast(FP8X4), scales=wk_s[e][:], in_=wk_bf[e][:])
 
-        q_s = gather(table_s["q"], tile([P, E * C], U8, "q_s"), 0, E)
-        q_w = gather(table_w["q"], tile([P, E * C], U32, "q_w"), 0, E)
-        k_w = gather(table_w["k"], tile([P, E * C], U32, "k_w"), 0, E)
-        k_s = gather(table_s["k"], tile([P, E * C], U8, "k_s"), 0, E)
-        v_w = [gather(table_w["v"], tile([P, C], U32, "v_w0"), 0, 1)]
+        q_s = gather(table_s["q"], tile([P, E * C], U8, "q_s"), 0, E * C)
+        q_w = gather(table_w["q"], tile([P, E * C], U32, "q_w"), 0, E * C)
+        k_w = gather(table_w["k"], tile([P, E * C], U32, "k_w"), 0, E * C)
+        k_s = gather(table_s["k"], tile([P, E * C], U8, "k_s"), 0, E * C)
+        v_w = [gather(table_w["v"], tile([P, C], U32, "v_w0"), 0, C)]
         round_wk(0)
         quantize_wk(0)
-        v_s = [gather(table_s["v"], tile([P, C], U8, "wk_raw0"), 0, 1)]
+        v_s = [[gather(table_s["v"], tile([P, C], U8, "wk_raw0"), 0, C)]]
         round_wk(1)
 
         def products(e, order):
@@ -140,7 +140,12 @@ def tile_moe_qkb_kernel(tc, dq_words, dq_scales, dk_words, dk_scales, dv_words, 
                     elif g == "k":
                         weights, weight_scales, words, scales = wk_w[e][:, cols].bitcast(FP8X4), wk_s[e][:, cols], k_w[:, slots], k_s[FIRST_ROW["k"] :, slots]
                     else:
-                        weights, weight_scales, words, scales = wv_w[e][:, 2 * b * P : 2 * (b + 1) * P].bitcast(FP4X4), wv_s[:, e, cols], v_w[e][:], v_s[e][:]
+                        width = C // len(v_s[e])
+                        for i, part in enumerate(v_s[e]):
+                            sub = slice(i * width, (i + 1) * width)
+                            nc.tensor.matmul_mx(out=sums[b][:, sub], lhsT=wv_w[e][:, 2 * b * P : 2 * (b + 1) * P].bitcast(FP4X4), lhsT_scale=wv_s[:, e, cols],
+                                                rhs=v_w[e][:, sub].bitcast(FP8X4), rhs_scale=part[:], start=False, stop=g == order[-1])
+                        continue
                     nc.tensor.matmul_mx(out=sums[b][:], lhsT=weights, lhsT_scale=weight_scales, rhs=words.bitcast(FP8X4), rhs_scale=scales,
                                         start=g == order[0], stop=g == order[-1])
             return sums
@@ -156,16 +161,17 @@ def tile_moe_qkb_kernel(tc, dq_words, dq_scales, dk_words, dk_scales, dv_words, 
             nc.vector.tensor_tensor(result[1][:].indirect(entries(lo, hi)), dx_high[:, lo:hi], gates[:, lo:hi], MULT)
 
         first = products(0, "qkv")
-        v_w.append(gather(table_w["v"], tile([P, C], U32, "wq_w0"), 1, 2))
+        v_w.append(gather(table_w["v"], tile([P, C], U32, "wq_w0"), C, 2 * C))
+        v_s.append([gather(table_s["v"], tile([P, P], U8, "wk_bf0"), C, C + P)])
         nc.scalar.copy(dx_high[:, 0:C], first[1][:])
         low_band(0, first[0])
-        v_s.append(gather(table_s["v"], tile([P, C], U8, "wv_w0"), 1, 2))
+        v_s[1].append(gather(table_s["v"], tile([P, P], U8, "wv_w0"), C + P, 2 * C))
         wk_s.append(tile([P, K], U8, "v_w0"))
         quantize_wk(1)
         high_band(0, P)
         second = products(1, "qvk")
-        nc.scalar.copy(dx_high[:, C : 2 * C], second[1][:])
         low_band(1, second[0])
+        nc.vector.tensor_copy(dx_high[:, C : 2 * C], second[1][:])
         high_band(P, E * C)
         for b in range(BANDS):
             nc.sync.dma_start(out=out[b * P : (b + 1) * P, :], in_=result[b][:])

@@ -151,27 +151,29 @@ def tile_moe_qkb_kernel(tc, dq_words, dq_scales, dk_words, dk_scales, dv_words, 
             return sums
 
         dx_low = [tile([P, C], F32, "dx_low%d" % e) for e in range(E)]
-        dx_high = tile([P, E * C], F32, "dx_high")
+        dx_cover = tile([P, P], F32, "dx_cover")
 
         def low_band(e, sums):
             nc.vector.tensor_tensor(dx_low[e][:], sums[:], gates[:, e * C : (e + 1) * C], MULT)
             nc.scalar.activation(result[0][:].indirect(entries(e * C, (e + 1) * C)), dx_low[e][:], COPY)
 
-        def high_band(lo, hi):
-            nc.vector.tensor_tensor(result[1][:].indirect(entries(lo, hi)), dx_high[:, lo:hi], gates[:, lo:hi], MULT)
+        def high_band(dx, lo, hi):
+            nc.vector.tensor_tensor(result[1][:].indirect(entries(lo, hi)), dx[:], gates[:, lo:hi], MULT)
 
         first = products(0, "qkv")
         v_w.append(gather(table_w["v"], tile([P, C], U32, "wq_w0"), C, 2 * C))
         v_s.append([gather(table_s["v"], tile([P, P], U8, "wk_bf0"), C, C + P)])
-        nc.scalar.copy(dx_high[:, 0:C], first[1][:])
+        nc.scalar.copy(dx_cover[:], first[1][:, 0:P])
         low_band(0, first[0])
         v_s[1].append(gather(table_s["v"], tile([P, P], U8, "wv_w0"), C + P, 2 * C))
         wk_s.append(tile([P, K], U8, "v_w0"))
         quantize_wk(1)
-        high_band(0, P)
+        high_band(dx_cover, 0, P)
+        dx_rest = tile([P, E * C - P], F32, "wk_bf1")
+        nc.scalar.copy(dx_rest[:, 0:P], first[1][:, P:C])
         second = products(1, "qvk")
         low_band(1, second[0])
-        nc.vector.tensor_copy(dx_high[:, C : 2 * C], second[1][:])
-        high_band(P, E * C)
+        nc.vector.tensor_copy(dx_rest[:, P : P + C], second[1][:])
+        high_band(dx_rest, P, E * C)
         for b in range(BANDS):
             nc.sync.dma_start(out=out[b * P : (b + 1) * P, :], in_=result[b][:])

@@ -84,17 +84,18 @@ def tile_moe_qkb_kernel(tc, dq_words, dq_scales, dk_words, dk_scales, dv_words, 
         load_weight_scales(nc.gpsimd, wq_s, wq_scales, FIRST_ROW["wq"])
         load_weight_scales(nc.gpsimd, wv_s, wv_scales, FIRST_ROW["wv"], range(0, 2))
         load_table_words("q", dq_words)
+        load_weight_scales(nc.sync, wv_s, wv_scales, FIRST_ROW["wv"], range(2, 3))
         load_table_words("k", dk_words)
         load_table_scales(nc.sync, "k", dk_scales)
-        load_table_scales(nc.sync, "v", dv_scales, range(0, 1))
         load_wk(0)
+        load_table_scales(nc.sync, "v", dv_scales, range(0, 1))
         load_table_words("v", dv_words)
         load_table_scales(nc.sync, "v", dv_scales, range(1, 4))
         load_wq(0)
         load_wk(1)
         load_gate(0)
         load_wv(0)
-        load_weight_scales(nc.sync, wv_s, wv_scales, FIRST_ROW["wv"], range(2, 4))
+        load_weight_scales(nc.sync, wv_s, wv_scales, FIRST_ROW["wv"], range(3, 4))
         load_wq(1)
         load_wv(1)
         load_gate(1)

@@ -82,9 +82,9 @@ def tile_moe_qkb_kernel(tc, dq_words, dq_scales, dk_words, dk_scales, dv_words, 
             queue.dma_start(out=table_s["q"][q * QUAD : (q + 1) * QUAD, :].bitcast(I32), in_=rows.unsqueeze(0).to_broadcast([QUAD // 4, 4, T // 4]))
         nc.sync.dma_start(offsets[:], offs)
         load_weight_scales(nc.gpsimd, wq_s, wq_scales, FIRST_ROW["wq"])
-        load_weight_scales(nc.gpsimd, wv_s, wv_scales, FIRST_ROW["wv"], range(0, 2))
+        load_weight_scales(nc.gpsimd, wv_s, wv_scales, FIRST_ROW["wv"], range(0, 1))
         load_table_words("q", dq_words)
-        load_weight_scales(nc.sync, wv_s, wv_scales, FIRST_ROW["wv"], range(2, 3))
+        load_weight_scales(nc.sync, wv_s, wv_scales, FIRST_ROW["wv"], range(1, 2))
         load_table_words("k", dk_words)
         load_table_scales(nc.sync, "k", dk_scales)
         load_wk(0)
@@ -95,7 +95,7 @@ def tile_moe_qkb_kernel(tc, dq_words, dq_scales, dk_words, dk_scales, dv_words, 
         load_wk(1)
         load_gate(0)
         load_wv(0)
-        load_weight_scales(nc.sync, wv_s, wv_scales, FIRST_ROW["wv"], range(3, 4))
+        load_weight_scales(nc.sync, wv_s, wv_scales, FIRST_ROW["wv"], range(2, 4))
         load_wq(1)
         load_wv(1)
         load_gate(1)

from contextlib import ExitStack

import concourse.mybir as mybir

K, T, E, C, N = 256, 1024, 2, 256, 512
FLOPS = 3 * 2 * N * K * E * C

F32 = mybir.dt.float32
BF16 = mybir.dt.bfloat16
I32 = mybir.dt.int32
U32 = mybir.dt.uint32
U16 = mybir.dt.uint16
U8 = mybir.dt.uint8
FP8X4 = mybir.dt.float8_e4m3fn_x4
FP4X4 = mybir.dt.float4_e2m1fn_x4
MULT = mybir.AluOpType.mult
COPY = mybir.ActivationFunctionType.Copy

P = 128
PACK = 4
QUAD = 32
BANDS = K // P
FIRST_ROW = {"q": 4, "k": 12, "v": 0, "wq": 8, "wv": 0}


def tile_moe_qkb_kernel(tc, dq_words, dq_scales, dk_words, dk_scales, dv_words, dv_scales, wq_words, wq_scales, wk, wv_words, wv_scales, gate, offs, out):
    nc = tc.nc
    with ExitStack() as ctx:
        keep = ctx.enter_context(tc.tile_pool(name="keep", bufs=1))
        psum = ctx.enter_context(tc.psum_pool(name="psum", bufs=1))

        def tile(shape, dtype, name):
            return keep.tile(shape, dtype, name=name, align_bytes=64)

        offsets = keep.tile([P, E * C // 16], U16, name="offsets")
        table_w = {g: tile([P, T], U32, "table_w_" + g) for g in "qkv"}
        table_s = {g: tile([P, T], U8, "table_s_" + g) for g in "qkv"}
        wq_w = [tile([P, K], U32, "wq_w%d" % e) for e in range(E)]
        wq_s = tile([P, E, K], U8, "wq_s")
        wv_w = [tile([P, 2 * K], U8, "wv_w%d" % e) for e in range(E)]
        wv_s = tile([P, E, K], U8, "wv_s")
        wk_raw = [tile([P, PACK, K], F32, "wk_raw%d" % e) for e in range(E)]
        wk_bf = [tile([P, K * PACK], BF16, "wk_bf%d" % e) for e in range(E)]
        wk_w = [tile([P, K], U32, "wk_w%d" % e) for e in range(E)]
        wk_s = [tile([P, K], U8, "wk_s0")]
        gates = tile([P, E * C], F32, "gates")
        result = [tile([P, T], F32, "result%d" % b) for b in range(BANDS)]

        nc.vector.memset(table_s["k"][:].bitcast(I32), 0)
        nc.vector.memset(table_s["v"][:].bitcast(I32), 0)
        zero = tile([P, 1], F32, "zero")
        nc.vector.memset(zero[:], 0.0)

        def load_table_words(g, words):
            nc.sync.dma_start(out=table_w[g][:].bitcast(I32), in_=words[0].rearrange("p t d -> p (t d)").bitcast(I32))

        def load_table_scales(queue, g, scales, which=range(4)):
            rows = scales[0].rearrange("(q r) t -> r q t", r=4)
            for r in which:
                queue.dma_start(out=table_s[g][FIRST_ROW[g] + r : P : QUAD, :].bitcast(I32), in_=rows[r].bitcast(I32))

        def load_weight_scales(queue, plane, scales, first, which=range(4)):
            rows = scales.rearrange("e s (q r) c -> r q (e s) c", r=4)
            for r in which:
                queue.dma_start(out=plane[first + r : P : QUAD, :, :].bitcast(I32), in_=rows[r].bitcast(I32))

        def load_wk(e):
            nc.sync.dma_start(out=wk_raw[e][:], in_=wk[e].rearrange("(p j) c -> p j c", j=PACK))

        def load_wq(e):
            nc.sync.dma_start(out=wq_w[e][:].bitcast(I32), in_=wq_words[e, 0].rearrange("p c d -> p (c d)").bitcast(I32))

        def load_wv(e):
            nc.sync.dma_start(out=wv_w[e][:].bitcast(I32), in_=wv_words[e, 0].bitcast(I32))

        def load_gate(e):
            nc.sync.dma_start(out=gates[:, e * C : (e + 1) * C], in_=gate[:, e * C : (e + 1) * C])

        for q in range(P // QUAD):
            rows = dq_scales[0, 4 * q : 4 * q + 4, :].bitcast(I32)
            queue = nc.sync if q < 2 else nc.scalar
            queue.dma_start(out=table_s["q"][q * QUAD : (q + 1) * QUAD, :].bitcast(I32), in_=rows.unsqueeze(0).to_broadcast([QUAD // 4, 4, T // 4]))
        nc.sync.dma_start(offsets[:], offs)
        load_weight_scales(nc.gpsimd, wq_s, wq_scales, FIRST_ROW["wq"])
        load_weight_scales(nc.gpsimd, wv_s, wv_scales, FIRST_ROW["wv"], range(0, 1))
        load_table_words("q", dq_words)
        load_weight_scales(nc.sync, wv_s, wv_scales, FIRST_ROW["wv"], range(1, 2))
        load_table_words("k", dk_words)
        load_table_scales(nc.sync, "k", dk_scales)
        load_wk(0)
        load_table_scales(nc.sync, "v", dv_scales, range(0, 1))
        load_table_words("v", dv_words)
        load_table_scales(nc.sync, "v", dv_scales, range(1, 4))
        load_wq(0)
        load_wk(1)
        load_gate(0)
        load_wv(0)
        load_weight_scales(nc.sync, wv_s, wv_scales, FIRST_ROW["wv"], range(2, 4))
        load_wq(1)
        load_wv(1)
        load_gate(1)

        for b in range(BANDS):
            nc.scalar.activation(result[b][:], zero[:].to_broadcast([P, T]), COPY)

        def entries(lo, hi):
            return offsets[:, lo // 16 : hi // 16]

        def gather(table, slots, lo, hi):
            nc.vector.tensor_copy(slots[:], table[:].indirect(entries(lo, hi)))
            return slots

        def round_wk(e):
            nc.scalar.activation(
                out=wk_bf[e][:].rearrange("p (c i j) -> p c j i", i=4, j=PACK),
                in_=wk_raw[e][:].rearrange("p j (c i) -> p c j i", i=4),
                func=COPY,
            )

        def quantize_wk(e):
            nc.vector.quantize_mx(out=wk_w[e][:].bitcast(FP8X4), scales=wk_s[e][:], in_=wk_bf[e][:])

        q_s = gather(table_s["q"], tile([P, E * C], U8, "q_s"), 0, E * C)
        q_w = gather(table_w["q"], tile([P, E * C], U32, "q_w"), 0, E * C)
        k_w = gather(table_w["k"], tile([P, E * C], U32, "k_w"), 0, E * C)
        k_s = gather(table_s["k"], tile([P, E * C], U8, "k_s"), 0, E * C)
        v_w = [gather(table_w["v"], tile([P, C], U32, "v_w0"), 0, C)]
        round_wk(0)
        quantize_wk(0)
        v_s = [[gather(table_s["v"], tile([P, C], U8, "wk_raw0"), 0, C)]]
        round_wk(1)

        def products(e, order):
            slots = slice(e * C, (e + 1) * C)
            sums = [psum.tile([P, C], F32, name="sums%d_%d" % (e, b)) for b in range(BANDS)]
            for g in order:
                for b in range(BANDS):
                    cols = slice(b * P, (b + 1) * P)
                    if g == "q":
                        weights, weight_scales, words, scales = wq_w[e][:, cols].bitcast(FP8X4), wq_s[FIRST_ROW["wq"] :, e, cols], q_w[:, slots], q_s[FIRST_ROW["q"] :, slots]
                    elif g == "k":
                        weights, weight_scales, words, scales = wk_w[e][:, cols].bitcast(FP8X4), wk_s[e][:, cols], k_w[:, slots], k_s[FIRST_ROW["k"] :, slots]
                    else:
                        width = C // len(v_s[e])
                        for i, part in enumerate(v_s[e]):
                            sub = slice(i * width, (i + 1) * width)
                            nc.tensor.matmul_mx(out=sums[b][:, sub], lhsT=wv_w[e][:, 2 * b * P : 2 * (b + 1) * P].bitcast(FP4X4), lhsT_scale=wv_s[:, e, cols],
                                                rhs=v_w[e][:, sub].bitcast(FP8X4), rhs_scale=part[:], start=False, stop=g == order[-1])
                        continue
                    nc.tensor.matmul_mx(out=sums[b][:], lhsT=weights, lhsT_scale=weight_scales, rhs=words.bitcast(FP8X4), rhs_scale=scales,
                                        start=g == order[0], stop=g == order[-1])
            return sums

        dx_low = [tile([P, C], F32, "dx_low%d" % e) for e in range(E)]
        dx_cover = tile([P, P], F32, "dx_cover")

        def low_band(e, sums):
            nc.vector.tensor_tensor(dx_low[e][:], sums[:], gates[:, e * C : (e + 1) * C], MULT)
            nc.scalar.activation(result[0][:].indirect(entries(e * C, (e + 1) * C)), dx_low[e][:], COPY)

        def high_band(dx, lo, hi):
            nc.vector.tensor_tensor(result[1][:].indirect(entries(lo, hi)), dx[:], gates[:, lo:hi], MULT)

        first = products(0, "qkv")
        v_w.append(gather(table_w["v"], tile([P, C], U32, "wq_w0"), C, 2 * C))
        v_s.append([gather(table_s["v"], tile([P, P], U8, "wk_bf0"), C, C + P)])
        nc.scalar.copy(dx_cover[:], first[1][:, 0:P])
        low_band(0, first[0])
        v_s[1].append(gather(table_s["v"], tile([P, P], U8, "wv_w0"), C + P, 2 * C))
        wk_s.append(tile([P, K], U8, "v_w0"))
        quantize_wk(1)
        high_band(dx_cover, 0, P)
        dx_rest = tile([P, E * C - P], F32, "wk_bf1")
        nc.scalar.copy(dx_rest[:, 0:P], first[1][:, P:C])
        second = products(1, "qvk")
        low_band(1, second[0])
        nc.vector.tensor_copy(dx_rest[:, P : P + C], second[1][:])
        high_band(dx_rest, P, E * C)
        for b in range(BANDS):
            nc.sync.dma_start(out=out[b * P : (b + 1) * P, :], in_=result[b][:])
